import numpy as np
import ml_dtypes


def mxq(x, axis, fmt="e4m3"):
    dtype, down = {"e4m3": (ml_dtypes.float8_e4m3fn, 7), "e5m2": (ml_dtypes.float8_e5m2, 14)}[fmt]
    v = np.moveaxis(np.asarray(x, np.float32).astype(ml_dtypes.bfloat16).astype(np.float64), axis, -1)
    blocks = v.reshape(v.shape[:-1] + (-1, 32))
    amax = np.abs(blocks).max(-1, keepdims=True)
    byte = np.maximum(np.where(amax > 0, np.frexp(amax)[1] - 1 + 127, 0) - down, 1)
    scale = np.exp2(byte - 127.0)
    codes = (blocks / scale).astype(np.float32).astype(dtype).astype(np.float64)
    return np.moveaxis((codes * scale).reshape(v.shape), -1, axis)


WIDE = False


def mx_kscale(k):
    if not WIDE:
        return np.ones(k)
    levels = np.array([10, -10, 5, -5, 0])
    if k % 512:
        return np.exp2(np.random.permutation(np.resize(levels, k // 32))).repeat(32)
    a = np.empty((k // 512, 16))
    for p in range(k // 512):
        a[p, :8] = np.random.permutation(np.resize(levels, 8))
        for g in range(8):
            far = levels[np.abs(levels - a[p, g]) >= 10]
            a[p, g + 8] = far[np.random.randint(len(far))]
    return np.exp2(a.ravel()).repeat(32)


def f64(x):
    return np.asarray(x).astype(np.float64)


def striped(idx):
    return np.tile(idx.reshape(-1, 16).T, (8, 1)).astype(np.uint16)


def unstriped(offs):
    return offs[:16].T.reshape(-1).astype(np.int64)


def striped8(idx):
    return np.concatenate([x.reshape(-1, 16).T for x in idx]).astype(np.uint16)


def runs(offs, k):
    lists = np.stack([offs[16 * r : 16 * r + 16].T.reshape(-1) for r in range(8)]).astype(np.int64)
    return lists[np.arange(k) % 512 // 64]


def pack_weight(w):
    k, n = w.shape
    w = f64(np.asarray(w, np.float32).astype(ml_dtypes.bfloat16)).reshape(k // 32, 32, n)
    amax = np.abs(w).max(1)
    byte = np.clip(np.where(amax > 0, np.frexp(amax)[1] - 1 + 127 - 7, 1), 1, 254)
    scaled = (w * np.exp2(127.0 - byte)[:, None, :]).reshape(k, n).astype(np.float32)
    words = np.ascontiguousarray(scaled.reshape(k // 512, 128, 4, n).transpose(0, 1, 3, 2)).astype(ml_dtypes.float8_e4m3fn).view(np.uint8)
    return words, np.ascontiguousarray(byte.astype(np.uint8).reshape(k // 512, 16, n))


def unpack_weight(words, scales):
    g, p, n, _ = words.shape
    vals = np.ascontiguousarray(words).view(ml_dtypes.float8_e4m3fn).astype(np.float64) * np.repeat(np.exp2(scales.astype(np.float64) - 127.0), 8, axis=1)[..., None]
    return vals.transpose(0, 1, 3, 2).reshape(g * 512, n)


E2M1 = np.array([0.0, 0.5, 1.0, 1.5, 2.0, 3.0, 4.0, 6.0, -0.0, -0.5, -1.0, -1.5, -2.0, -3.0, -4.0, -6.0])


def pack_fp4(w):
    k, n = w.shape
    w = f64(np.asarray(w, np.float32).astype(ml_dtypes.bfloat16)).reshape(k // 32, 32, n)
    amax = np.abs(w).max(1)
    mant, ex = np.frexp(amax / 6.0)
    byte = np.clip(np.where(amax > 0, np.where(mant > 0.5, ex, ex - 1) + 127, 1), 1, 254)
    scaled = (w * np.exp2(127.0 - byte)[:, None, :]).reshape(k, n).astype(np.float32)
    c = np.ascontiguousarray(scaled.reshape(k // 512, 128, 4, n).transpose(0, 1, 3, 2)).astype(ml_dtypes.float4_e2m1fn).view(np.uint8) & 0xF
    words = (c[..., 0::2] | (c[..., 1::2] << 4)).reshape(k // 512, 128, 2 * n)
    return np.ascontiguousarray(words), np.ascontiguousarray(byte.astype(np.uint8).reshape(k // 512, 16, n))


def unpack_fp4(words, scales):
    g, _, n = scales.shape
    words = np.ascontiguousarray(words).reshape(g, 128, n, 2)
    nib = np.empty((g, 128, n, 4), np.uint8)
    nib[..., 0::2] = words & 0xF
    nib[..., 1::2] = words >> 4
    vals = E2M1[nib] * np.repeat(np.exp2(scales.astype(np.float64) - 127.0), 8, axis=1)[..., None]
    return vals.transpose(0, 1, 3, 2).reshape(g * 512, n)


def gelu(v):
    return 0.5 * v * (1.0 + np.tanh(np.sqrt(2.0 / np.pi) * (v + 0.044715 * v**3)))

def planes(y):
    n, m = y.shape
    v = y.astype(np.float32).astype(ml_dtypes.bfloat16).astype(np.float64).reshape(n // 32, 32, m)
    top = np.abs(v).max(1)
    byte = np.clip(np.where(top > 0, np.frexp(top)[1] - 1 + 127 - 7, 1), 1, 254)
    codes = (v * np.exp2(127.0 - byte)[:, None, :]).reshape(n, m).astype(np.float32).astype(ml_dtypes.float8_e4m3fn).view(np.uint8)
    words = codes.reshape(n // 512, 128, 4, m).transpose(0, 1, 3, 2)
    return np.ascontiguousarray(words), np.ascontiguousarray(byte.astype(np.uint8).reshape(n // 512, 16, m))


K, T, S, N, H = 512, 2048, 512, 512, 512
P = 2 ** 7


def setup_inputs():
    n = np.random.standard_normal
    s = mx_kscale(K)[:, None]
    u = mx_kscale(H)
    packed_xT = pack_weight(n((K, T)) * s)
    packed_w2 = pack_fp4(n((H, N)) / np.sqrt(H) / u[:, None])
    return {
        "x_words": packed_xT[0],
        "x_scales": packed_xT[1],
        "w1": (n((K, H)) / np.sqrt(K) / s * u).astype(np.float32),
        "ga": np.tile(np.random.uniform(0.2, 1.0, S), (P, 1)).astype(np.float32),
        "w2_words": packed_w2[0],
        "w2_scales": packed_w2[1],
        "offs": striped(np.random.permutation(T)[:S]),
        "p1": striped8(np.stack([np.random.permutation(S) for _ in range(8)])),
        "p2": striped8(np.stack([np.random.permutation(S) for _ in range(8)])),
        "q1": striped8(np.stack([np.random.permutation(S) for _ in range(8)])),
    }


def reference(x_words, x_scales, w1, ga, w2_words, w2_scales, offs, p1, p2, q1):
    xq = unpack_weight(x_words, x_scales)[:, unstriped(offs)]
    y = mxq(f64(w1), 0, "e4m3").T @ xq
    h = y + f64(ga)[:1] * (y[np.arange(H)[:, None], runs(p1, H)] + y[np.arange(H)[:, None], runs(p2, H)])
    z = gelu(h - (h[np.arange(H)[:, None], runs(q1, H)]))
    out_0 = unpack_fp4(w2_words, w2_scales).T @ mxq(z, 0, "e4m3")
    return (out_0,) + planes(out_0)

@@ -1,0 +1,232 @@
+from contextlib import ExitStack
+
+import concourse.mybir as mybir
+from concourse.masks import make_identity
+
+F32 = mybir.dt.float32
+BF16 = mybir.dt.bfloat16
+I32 = mybir.dt.int32
+U32 = mybir.dt.uint32
+U16 = mybir.dt.uint16
+U8 = mybir.dt.uint8
+FP8X4 = mybir.dt.float8_e4m3fn_x4
+FP4X4 = mybir.dt.float4_e2m1fn_x4
+ALU = mybir.AluOpType
+ACT = mybir.ActivationFunctionType
+
+P = 128
+T = 2048
+S = 512
+H = 512
+FLOPS = 2 * 2 * 512 * 512 * 512
+PE_TILES = 3
+WARM = True
+CHUNKS = [128,128,128,128]
+CAST_ON_SCALAR = []
+
+
+def tile_picked_twohop8_gelu_po_kernel(tc, x_words, x_scales, w1, ga, w2_words, w2_scales, offs, p1, p2, q1, out_0, out_1, out_2):
+    nc = tc.nc
+    with ExitStack() as ctx:
+        keep = ctx.enter_context(tc.tile_pool(name="keep", bufs=1))
+        psum = ctx.enter_context(tc.psum_pool(name="psum", bufs=2))
+
+        def sb(shape, dtype, name):
+            return keep.tile(shape, dtype, name=name, align_bytes=64)
+
+        offs_sb = keep.tile([P, S // 16], U16, name="offs_sb")
+        p1_sb = keep.tile([P, S // 16], U16, name="p1_sb")
+        p2_sb = keep.tile([P, S // 16], U16, name="p2_sb")
+        q1_sb = keep.tile([P, S // 16], U16, name="q1_sb")
+
+        xs_all = sb([P, T], U8, "xs_all")
+        xw_all = sb([P, T], U32, "xw_all")
+        w2s_raw = sb([P, H], U8, "w2s_raw")
+        w2w_raw = sb([P, 2 * H], U8, "w2w_raw")
+        ga_sb = sb([P, S], F32, "ga_sb")
+        w1_raw = [sb([P, 4, 256], F32, "w1_raw%d" % u) for u in range(2)]
+
+        nc.vector.memset(xs_all[:].bitcast(I32), 0)
+        nc.gpsimd.memset(w2s_raw[:].bitcast(I32), 0)
+        if WARM:
+            warm = sb([P, 2], F32, "warm")
+            nc.vector.memset(warm[:, 0:1], 0.0)
+
+        w1_v = w1.rearrange("(p j) c -> p j c", j=4)
+        nc.sync.dma_start(offs_sb[:], offs)
+        for q in range(4):
+            nc.scalar.dma_start(out=xs_all[32 * q : 32 * q + 4, :].bitcast(I32), in_=x_scales[0][4 * q : 4 * q + 4, :].bitcast(I32))
+        if WARM:
+            nc.scalar.activation(out=warm[:, 1:2], in_=warm[:, 0:1], func=ACT.Gelu_apprx_tanh)
+        nc.sync.dma_start(out=w2w_raw[:].bitcast(I32), in_=w2_words[0].bitcast(I32))
+        for u in range(2):
+            nc.sync.dma_start(out=w1_raw[u][:], in_=w1_v[:, :, 256 * u : 256 * (u + 1)])
+        nc.sync.dma_start(out=xw_all[:].bitcast(I32), in_=x_words[0].rearrange("p c r -> p (c r)").bitcast(I32))
+        nc.sync.dma_start(p1_sb[:], p1)
+        nc.sync.dma_start(out=ga_sb[:], in_=ga)
+        nc.sync.dma_start(p2_sb[:], p2)
+        for q in range(4):
+            nc.sync.dma_start(out=w2s_raw[32 * q : 32 * q + 4, :].bitcast(I32), in_=w2_scales[0][4 * q : 4 * q + 4, :].bitcast(I32))
+        nc.sync.dma_start(q1_sb[:], q1)
+
+        if PE_TILES:
+            ident = sb([P, P], F32, "ident")
+            make_identity(nc, ident[:])
+
+        xs = sb([P, S], U8, "xs")
+        nc.vector.tensor_copy(out=xs[:], in_=xs_all[:].indirect(offs_sb[:]))
+        w2w = sb([P, 2 * H], U8, "w2w")
+        nc.vector.tensor_copy(
+            out=w2w[:].rearrange("p (t m b) -> p t m b", t=4, b=2),
+            in_=w2w_raw[:].rearrange("p (m t b) -> p t m b", t=4, b=2),
+        )
+
+        w1_bf = sb([P, 4 * H], BF16, "w1_bf")
+        w1_bf_v = w1_bf[:].rearrange("p (t m j) -> p m t j", t=4, j=4)
+        nc.scalar.copy(out=w1_bf_v[:, 0:64], in_=w1_raw[0][:].rearrange("p j (m t) -> p m t j", t=4))
+        nc.vector.tensor_copy(out=w1_bf_v[:, 64:128], in_=w1_raw[1][:].rearrange("p j (m t) -> p m t j", t=4))
+        w1c = sb([P, H], U32, "w1c")
+        w1s = sb([P, H], U8, "w1s")
+        nc.vector.quantize_mx(out=w1c[:].bitcast(FP8X4), scales=w1s[:], in_=w1_bf[:])
+
+        xw = sb([P, S], U32, "xw")
+        for u in range(2):
+            nc.vector.tensor_copy(out=xw[:, 256 * u : 256 * (u + 1)], in_=xw_all[:].indirect(offs_sb[:, 16 * u : 16 * (u + 1)]))
+        w2s = sb([P, H], U8, "w2s")
+        nc.vector.tensor_copy(out=w2s[:].rearrange("p (t m) -> p t m", t=4), in_=w2s_raw[:].rearrange("p (m t) -> p t m", t=4))
+
+        y = [sb([P, S], F32, "y%d" % t) for t in range(4)]
+        pieces = [(0, 0, 256), (0, 256, 512)] + [(t, 0, 512) for t in range(1, 4)]
+        for t, a, b in pieces:
+            acc = psum.tile([P, S], F32, name="acc", tag="mm", bufs=4)
+            nc.tensor.matmul_mx(
+                out=acc[:, 0 : b - a],
+                lhsT=w1c[:, P * t : P * (t + 1)].bitcast(FP8X4),
+                lhsT_scale=w1s[:, P * t : P * (t + 1)],
+                rhs=xw[:, a:b].bitcast(FP8X4),
+                rhs_scale=xs[:, a:b],
+                start=True,
+                stop=True,
+            )
+            nc.scalar.copy(out=y[t][:, a:b], in_=acc[:, 0 : b - a])
+
+        h = [sb([P, S], F32, "h%d" % t) for t in range(4)]
+        starts = [sum(CHUNKS[:c]) for c in range(len(CHUNKS))]
+        LATE = PE_TILES - 1
+        h2 = [sb([P, S], F32, "h2_%d" % t) if t < LATE else None for t in range(4)]
+        late = [keep.tile([P, n], F32, name="late%d" % c, tag="turn%d" % (c + 1), align_bytes=64) for c, n in enumerate(CHUNKS)]
+
+        def hop1(dst, t, lst, u):
+            cols = slice(256 * u, 256 * (u + 1))
+            nc.vector.tensor_tensor(dst[:, cols], y[t][:].indirect(lst[:, 16 * u : 16 * (u + 1)]), ga_sb[:, cols], ALU.mult)
+
+        for t in range(4):
+            m1 = sb([P, S], F32, "m1_%d" % t)
+            m2 = sb([P, S], F32, "m2_%d" % t)
+            if t < PE_TILES:
+                for u in range(2):
+                    hop1(m1, t, p1_sb, u)
+                for u in range(2):
+                    hop1(m2, t, p2_sb, u)
+                ht = psum.tile([P, 4, P], F32, name="ht", tag="ht", bufs=2)
+                for n, term in enumerate((y[t], m1, m2)):
+                    for b in range(4):
+                        nc.tensor.matmul(ht[:, b, :], term[:, P * b : P * (b + 1)], ident[:], is_transpose=True, start=(n == 0 and b == 0), stop=(n == 2 and b == 3))
+                ht_sb = keep.tile([P, 4, P], F32, name="ht_sb%d" % t, tag="ht_sb%d" % t, align_bytes=64)
+                nc.scalar.copy(out=ht_sb[:], in_=ht[:])
+                hb = psum.tile([P, 4, P], F32, name="hb", tag="hb", bufs=2)
+                for b in range(4):
+                    nc.tensor.transpose(hb[:, b, :], ht_sb[:, b, :], ident[:])
+                nc.scalar.copy(out=h[t][:], in_=hb[:].rearrange("p b j -> p (b j)"))
+                if t == LATE:
+                    for c, n in enumerate(CHUNKS):
+                        nc.scalar.copy(out=late[c][:], in_=hb[:].rearrange("p b j -> p (b j)")[:, starts[c] : starts[c] + n])
+                else:
+                    nc.scalar.copy(out=h2[t][:], in_=hb[:].rearrange("p b j -> p (b j)"))
+            else:
+                part = sb([P, S], F32, "part%d" % t)
+                h2[t] = keep.tile([P, S], F32, name="h2_%d" % t, tag="ht_sb%d" % LATE, align_bytes=64)
+                hop1(m1, t, p1_sb, 0)
+                hop1(m1, t, p1_sb, 1)
+                hop1(m2, t, p2_sb, 0)
+                nc.vector.tensor_tensor(part[:], m1[:], y[t][:], ALU.add)
+                hop1(m2, t, p2_sb, 1)
+                for u in range(2):
+                    cols = slice(256 * u, 256 * (u + 1))
+                    nc.vector.tensor_tensor(h[t][:, cols], part[:, cols], m2[:, cols], ALU.add)
+                    nc.scalar.copy(out=h2[t][:, cols], in_=h[t][:, cols])
+
+        oc = sb([P, S], U32, "oc")
+        osc = sb([P, S], U8, "osc")
+        out0_v = out_0.rearrange("(p t) j -> p t j", t=4)
+        out1_v = out_1[0].rearrange("p c r -> p (c r)").bitcast(I32)
+
+        zc = [None] * len(CHUNKS)
+        zs = [None] * len(CHUNKS)
+        z = [None] * len(CHUNKS)
+        o_sb = [None] * len(CHUNKS)
+        ob = [None] * len(CHUNKS)
+
+        def hop2(c):
+            a, n = starts[c], CHUNKS[c]
+            nd = keep.tile([P, 4, n], F32, name="nd%d" % c, tag="turn%d" % c, align_bytes=64)
+            for t in [u for u in range(4) if u != LATE] + [LATE]:
+                own = late[c][:] if t == LATE else h2[t][:, a : a + n]
+                nc.vector.tensor_tensor(nd[:, t, :], h[t][:].indirect(q1_sb[:, a // 16 : (a + n) // 16]), own, ALU.subtract)
+            z[c] = sb([P, 4 * n], BF16, "z%d" % c)
+            nc.scalar.activation(
+                out=z[c][:].rearrange("p (g i t) -> p g t i", i=4, t=4),
+                in_=nd[:].rearrange("p t (g i) -> p g t i", i=4),
+                func=ACT.Gelu_apprx_tanh,
+                scale=-1.0,
+            )
+
+        def product(c):
+            a, n = starts[c], CHUNKS[c]
+            zc = sb([P, n], U32, "zc%d" % c)
+            zs = sb([P, n], U8, "zs%d" % c)
+            nc.vector.quantize_mx(out=zc[:].bitcast(FP8X4), scales=zs[:], in_=z[c][:])
+            o_sb[c] = sb([P, 4, n], F32, "o_sb%d" % c)
+            ob[c] = sb([P, 4 * n], BF16, "ob%d" % c)
+            per = 2 if c == len(CHUNKS) - 1 else S // n
+            for g in range(4 // per):
+                acc = psum.tile([P, per, n], F32, name="acc2", tag="mm", bufs=4)
+                for k in range(per):
+                    t = per * g + k
+                    nc.tensor.matmul_mx(
+                        out=acc[:, k, :],
+                        lhsT=w2w[:, 2 * P * t : 2 * P * (t + 1)].bitcast(FP4X4),
+                        lhsT_scale=w2s[:, P * t : P * (t + 1)],
+                        rhs=zc[:].bitcast(FP8X4),
+                        rhs_scale=zs[:],
+                        start=True,
+                        stop=True,
+                    )
+                if c == len(CHUNKS) - 1 and g == 1:
+                    nc.vector.tensor_copy(out=o_sb[c][:, per * g : per * (g + 1), :], in_=acc[:])
+                else:
+                    nc.scalar.copy(out=o_sb[c][:, per * g : per * (g + 1), :], in_=acc[:])
+            nc.sync.dma_start(out=out0_v[:, :, a : a + n], in_=o_sb[c][:])
+
+        def planes(c):
+            a, n = starts[c], CHUNKS[c]
+            dst = ob[c][:].rearrange("p (g i t) -> p g t i", i=4, t=4)
+            src = o_sb[c][:].rearrange("p t (g i) -> p g t i", i=4)
+            if c in CAST_ON_SCALAR:
+                nc.scalar.copy(out=dst, in_=src)
+            else:
+                nc.vector.tensor_copy(out=dst, in_=src)
+            nc.vector.quantize_mx(out=oc[:, a : a + n].bitcast(FP8X4), scales=osc[:, a : a + n], in_=ob[c][:])
+            nc.sync.dma_start(out=out1_v[:, a : a + n], in_=oc[:, a : a + n].bitcast(I32))
+
+        last = len(CHUNKS)
+        for c in range(last + 1):
+            if c < last:
+                hop2(c)
+            if 1 <= c <= last:
+                product(c - 1)
+        for c in range(last):
+            planes(c)
+        for q in range(4):
+            eng = nc.sync if q % 2 == 0 else nc.scalar
+            eng.dma_start(out=out_2[0][4 * q : 4 * q + 4, :].bitcast(I32), in_=osc[32 * q : 32 * q + 4, :].bitcast(I32))

@@ -29,6 +29,7 @@ def tile_picked_twohop8_gelu_po_kernel(tc, x_words, x_scales, w1, ga, w2_words, 
     nc = tc.nc
     with ExitStack() as ctx:
         keep = ctx.enter_context(tc.tile_pool(name="keep", bufs=1))
+        turns = ctx.enter_context(tc.tile_pool(name="turns", bufs=1))
         psum = ctx.enter_context(tc.psum_pool(name="psum", bufs=2))
 
         def sb(shape, dtype, name):
@@ -43,44 +44,42 @@ def tile_picked_twohop8_gelu_po_kernel(tc, x_words, x_scales, w1, ga, w2_words, 
         xw_all = sb([P, T], U32, "xw_all")
         w2s_raw = sb([P, H], U8, "w2s_raw")
         w2w_raw = sb([P, 2 * H], U8, "w2w_raw")
-        ga_sb = sb([P, S], F32, "ga_sb")
-        w1_raw = [sb([P, 4, 256], F32, "w1_raw%d" % u) for u in range(2)]
+        w1_raw = [keep.tile([P, 4, 256], F32, name="w1_raw%d" % u, tag="w1_raw%d" % u, align_bytes=64) for u in range(2)]
 
-        nc.vector.memset(xs_all[:].bitcast(I32), 0)
-        nc.gpsimd.memset(w2s_raw[:].bitcast(I32), 0)
-        if WARM:
-            warm = sb([P, 2], F32, "warm")
-            nc.vector.memset(warm[:, 0:1], 0.0)
-
+        nc.gpsimd.memset(xs_all[:].bitcast(I32), 0)
+        nc.vector.memset(w2s_raw[:].bitcast(I32), 0)
         w1_v = w1.rearrange("(p j) c -> p j c", j=4)
         nc.sync.dma_start(offs_sb[:], offs)
-        for q in range(4):
-            nc.scalar.dma_start(out=xs_all[32 * q : 32 * q + 4, :].bitcast(I32), in_=x_scales[0][4 * q : 4 * q + 4, :].bitcast(I32))
-        if WARM:
-            nc.scalar.activation(out=warm[:, 1:2], in_=warm[:, 0:1], func=ACT.Gelu_apprx_tanh)
+        nc.sync.dma_start(p1_sb[:], p1)
         nc.sync.dma_start(out=w2w_raw[:].bitcast(I32), in_=w2_words[0].bitcast(I32))
+        nc.sync.dma_start(p2_sb[:], p2)
+        nc.sync.dma_start(q1_sb[:], q1)
         for u in range(2):
             nc.sync.dma_start(out=w1_raw[u][:], in_=w1_v[:, :, 256 * u : 256 * (u + 1)])
         nc.sync.dma_start(out=xw_all[:].bitcast(I32), in_=x_words[0].rearrange("p c r -> p (c r)").bitcast(I32))
-        nc.sync.dma_start(p1_sb[:], p1)
+        for q in range(4):
+            nc.scalar.dma_start(out=xs_all[32 * q : 32 * q + 4, :].bitcast(I32), in_=x_scales[0][4 * q : 4 * q + 4, :].bitcast(I32))
+        ga_sb = sb([P, S], F32, "ga_sb")
         nc.sync.dma_start(out=ga_sb[:], in_=ga)
-        nc.sync.dma_start(p2_sb[:], p2)
         for q in range(4):
             nc.sync.dma_start(out=w2s_raw[32 * q : 32 * q + 4, :].bitcast(I32), in_=w2_scales[0][4 * q : 4 * q + 4, :].bitcast(I32))
-        nc.sync.dma_start(q1_sb[:], q1)
+        if WARM:
+            warm = sb([P, 2], F32, "warm")
+            nc.vector.memset(warm[:, 0:1], 0.0)
+            nc.scalar.activation(out=warm[:, 1:2], in_=warm[:, 0:1], func=ACT.Gelu_apprx_tanh)
 
         if PE_TILES:
             ident = sb([P, P], F32, "ident")
             make_identity(nc, ident[:])
 
-        xs = sb([P, S], U8, "xs")
-        nc.vector.tensor_copy(out=xs[:], in_=xs_all[:].indirect(offs_sb[:]))
         w2w = sb([P, 2 * H], U8, "w2w")
         nc.vector.tensor_copy(
             out=w2w[:].rearrange("p (t m b) -> p t m b", t=4, b=2),
             in_=w2w_raw[:].rearrange("p (m t b) -> p t m b", t=4, b=2),
         )
 
+        xs = sb([P, S], U8, "xs")
+        nc.vector.tensor_copy(out=xs[:], in_=xs_all[:].indirect(offs_sb[:]))
         w1_bf = sb([P, 4 * H], BF16, "w1_bf")
         w1_bf_v = w1_bf[:].rearrange("p (t m j) -> p m t j", t=4, j=4)
         nc.scalar.copy(out=w1_bf_v[:, 0:64], in_=w1_raw[0][:].rearrange("p j (m t) -> p m t j", t=4))
@@ -114,7 +113,7 @@ def tile_picked_twohop8_gelu_po_kernel(tc, x_words, x_scales, w1, ga, w2_words, 
         starts = [sum(CHUNKS[:c]) for c in range(len(CHUNKS))]
         LATE = PE_TILES - 1
         h2 = [sb([P, S], F32, "h2_%d" % t) if t < LATE else None for t in range(4)]
-        late = [keep.tile([P, n], F32, name="late%d" % c, tag="turn%d" % (c + 1), align_bytes=64) for c, n in enumerate(CHUNKS)]
+        late = [turns.tile([P, n], F32, name="late%d" % c, offset=2048 * (c + 1), align_bytes=64) for c, n in enumerate(CHUNKS)]
 
         def hop1(dst, t, lst, u):
             cols = slice(256 * u, 256 * (u + 1))
@@ -169,11 +168,11 @@ def tile_picked_twohop8_gelu_po_kernel(tc, x_words, x_scales, w1, ga, w2_words, 
 
         def hop2(c):
             a, n = starts[c], CHUNKS[c]
-            nd = keep.tile([P, 4, n], F32, name="nd%d" % c, tag="turn%d" % c, align_bytes=64)
+            nd = turns.tile([P, 4, n], F32, name="nd%d" % c, offset=2048 * c, align_bytes=64)
             for t in [u for u in range(4) if u != LATE] + [LATE]:
                 own = late[c][:] if t == LATE else h2[t][:, a : a + n]
                 nc.vector.tensor_tensor(nd[:, t, :], h[t][:].indirect(q1_sb[:, a // 16 : (a + n) // 16]), own, ALU.subtract)
-            z[c] = sb([P, 4 * n], BF16, "z%d" % c)
+            z[c] = turns.tile([P, 4 * n], BF16, name="z%d" % c, offset=2048 * (c + 2) + 512, align_bytes=64)
             nc.scalar.activation(
                 out=z[c][:].rearrange("p (g i t) -> p g t i", i=4, t=4),
                 in_=nd[:].rearrange("p t (g i) -> p g t i", i=4),
@@ -217,7 +216,9 @@ def tile_picked_twohop8_gelu_po_kernel(tc, x_words, x_scales, w1, ga, w2_words, 
             else:
                 nc.vector.tensor_copy(out=dst, in_=src)
             nc.vector.quantize_mx(out=oc[:, a : a + n].bitcast(FP8X4), scales=osc[:, a : a + n], in_=ob[c][:])
-            nc.sync.dma_start(out=out1_v[:, a : a + n], in_=oc[:, a : a + n].bitcast(I32))
+            if c >= len(CHUNKS) - 2:
+                a0 = a if c == len(CHUNKS) - 1 else 0
+                nc.sync.dma_start(out=out1_v[:, a0 : a + n], in_=oc[:, a0 : a + n].bitcast(I32))
 
         last = len(CHUNKS)
         for c in range(last + 1):

@@ -12,222 +12,250 @@ U8 = mybir.dt.uint8
 FP8X4 = mybir.dt.float8_e4m3fn_x4
 FP4X4 = mybir.dt.float4_e2m1fn_x4
 ALU = mybir.AluOpType
-ACT = mybir.ActivationFunctionType
+GELU = mybir.ActivationFunctionType.Gelu_apprx_tanh
 
 P = 128
+PACK = 4
 T = 2048
 S = 512
 H = 512
-FLOPS = 2 * 2 * 512 * 512 * 512
-PE_TILES = 3
-WARM = True
-CHUNKS = [128,128,128,128]
-CAST_ON_SCALAR = []
+HALF = S // 2
+LANES = 16
+QUADRANT = 32
+CHUNK = 128
+CHUNKS = S // CHUNK
+FLOPS = 2 * H * H * S * 2
+
+TURNED = 3
+PIECES = ((0, 2 * CHUNK), (2 * CHUNK, 3 * CHUNK), (3 * CHUNK, 4 * CHUNK))
+REGION = PACK * 2 * CHUNK * 4
 
 
-def tile_picked_twohop8_gelu_po_kernel(tc, x_words, x_scales, w1, ga, w2_words, w2_scales, offs, p1, p2, q1, out_0, out_1, out_2):
+def tile_picked_twohop8_gelu_po_kernel(
+    tc, x_words, x_scales, w1, ga, w2_words, w2_scales, offs, p1, p2, q1, out_0, out_1, out_2
+):
     nc = tc.nc
     with ExitStack() as ctx:
         keep = ctx.enter_context(tc.tile_pool(name="keep", bufs=1))
-        turns = ctx.enter_context(tc.tile_pool(name="turns", bufs=1))
+        shared = ctx.enter_context(tc.tile_pool(name="shared", bufs=1))
         psum = ctx.enter_context(tc.psum_pool(name="psum", bufs=2))
 
-        def sb(shape, dtype, name):
+        def own(shape, dtype, name):
             return keep.tile(shape, dtype, name=name, align_bytes=64)
 
-        offs_sb = keep.tile([P, S // 16], U16, name="offs_sb")
-        p1_sb = keep.tile([P, S // 16], U16, name="p1_sb")
-        p2_sb = keep.tile([P, S // 16], U16, name="p2_sb")
-        q1_sb = keep.tile([P, S // 16], U16, name="q1_sb")
+        def placed(shape, dtype, name, offset):
+            return shared.tile(shape, dtype, name=name, offset=offset, align_bytes=64)
 
-        xs_all = sb([P, T], U8, "xs_all")
-        xw_all = sb([P, T], U32, "xw_all")
-        w2s_raw = sb([P, H], U8, "w2s_raw")
-        w2w_raw = sb([P, 2 * H], U8, "w2w_raw")
-        w1_raw = [keep.tile([P, 4, 256], F32, name="w1_raw%d" % u, tag="w1_raw%d" % u, align_bytes=64) for u in range(2)]
+        def product_bank(shape, name):
+            return psum.tile(shape, F32, name=name, tag="product", bufs=4)
 
-        nc.gpsimd.memset(xs_all[:].bitcast(I32), 0)
-        nc.vector.memset(w2s_raw[:].bitcast(I32), 0)
-        w1_v = w1.rearrange("(p j) c -> p j c", j=4)
+        def scale_rows(tile, q):
+            return tile[QUADRANT * q : QUADRANT * q + PACK, :].bitcast(I32)
+
+        def entries(list_tile, a, b):
+            return list_tile[:, a // LANES : b // LANES]
+
+        offs_sb = keep.tile([P, S // LANES], U16, name="offs_sb")
+        p1_sb = keep.tile([P, S // LANES], U16, name="p1_sb")
+        p2_sb = keep.tile([P, S // LANES], U16, name="p2_sb")
+        q1_sb = keep.tile([P, S // LANES], U16, name="q1_sb")
+        x_scale_table = own([P, T], U8, "x_scale_table")
+        x_word_table = own([P, T], U32, "x_word_table")
+        w2_scale_raw = own([P, H], U8, "w2_scale_raw")
+        w2_word_raw = own([P, 2 * H], U8, "w2_word_raw")
+        w1_raw = [own([P, PACK, H // 2], F32, "w1_raw%d" % u) for u in range(2)]
+        ga_sb = own([P, S], F32, "ga_sb")
+
+        nc.gpsimd.memset(x_scale_table[:].bitcast(I32), 0)
+        nc.gpsimd.memset(w2_scale_raw[:].bitcast(I32), 0)
+        w1_rows = w1.rearrange("(p j) c -> p j c", j=PACK)
         nc.sync.dma_start(offs_sb[:], offs)
         nc.sync.dma_start(p1_sb[:], p1)
-        nc.sync.dma_start(out=w2w_raw[:].bitcast(I32), in_=w2_words[0].bitcast(I32))
+        nc.sync.dma_start(out=w2_word_raw[:].bitcast(I32), in_=w2_words[0].bitcast(I32))
         nc.sync.dma_start(p2_sb[:], p2)
         nc.sync.dma_start(q1_sb[:], q1)
         for u in range(2):
-            nc.sync.dma_start(out=w1_raw[u][:], in_=w1_v[:, :, 256 * u : 256 * (u + 1)])
-        nc.sync.dma_start(out=xw_all[:].bitcast(I32), in_=x_words[0].rearrange("p c r -> p (c r)").bitcast(I32))
-        for q in range(4):
-            nc.scalar.dma_start(out=xs_all[32 * q : 32 * q + 4, :].bitcast(I32), in_=x_scales[0][4 * q : 4 * q + 4, :].bitcast(I32))
-        ga_sb = sb([P, S], F32, "ga_sb")
+            nc.sync.dma_start(out=w1_raw[u][:], in_=w1_rows[:, :, u * H // 2 : (u + 1) * H // 2])
+        nc.sync.dma_start(out=x_word_table[:].bitcast(I32), in_=x_words[0].rearrange("p c r -> p (c r)").bitcast(I32))
+        for q in range(PACK):
+            nc.scalar.dma_start(out=scale_rows(x_scale_table, q), in_=x_scales[0][PACK * q : PACK * (q + 1), :].bitcast(I32))
         nc.sync.dma_start(out=ga_sb[:], in_=ga)
-        for q in range(4):
-            nc.sync.dma_start(out=w2s_raw[32 * q : 32 * q + 4, :].bitcast(I32), in_=w2_scales[0][4 * q : 4 * q + 4, :].bitcast(I32))
-        if WARM:
-            warm = sb([P, 2], F32, "warm")
-            nc.vector.memset(warm[:, 0:1], 0.0)
-            nc.scalar.activation(out=warm[:, 1:2], in_=warm[:, 0:1], func=ACT.Gelu_apprx_tanh)
+        for q in range(PACK):
+            queue = nc.sync if q < PACK // 2 else nc.gpsimd
+            queue.dma_start(out=scale_rows(w2_scale_raw, q), in_=w2_scales[0][PACK * q : PACK * (q + 1), :].bitcast(I32))
 
-        if PE_TILES:
-            ident = sb([P, P], F32, "ident")
-            make_identity(nc, ident[:])
+        zero = own([P, 2], F32, "zero")
+        nc.vector.memset(zero[:, 0:1], 0.0)
+        nc.scalar.activation(out=zero[:, 1:2], in_=zero[:, 0:1], func=GELU)
 
-        w2w = sb([P, 2 * H], U8, "w2w")
+        identity = own([P, P], F32, "identity")
+        make_identity(nc, identity[:])
+
+        y = [own([P, 2 * S], F32, "y%d" % t) for t in range(PACK)]
+        for t in range(PACK):
+            nc.vector.memset(y[t][:, S : 2 * S], 0.0)
+
+        w2_word = own([P, 2 * H], U8, "w2_word")
         nc.vector.tensor_copy(
-            out=w2w[:].rearrange("p (t m b) -> p t m b", t=4, b=2),
-            in_=w2w_raw[:].rearrange("p (m t b) -> p t m b", t=4, b=2),
+            out=w2_word[:].rearrange("p (t m b) -> p t m b", t=PACK, b=2),
+            in_=w2_word_raw[:].rearrange("p (m t b) -> p t m b", t=PACK, b=2),
+        )
+        x_scale = own([P, S], U8, "x_scale")
+        nc.vector.tensor_copy(out=x_scale[:], in_=x_scale_table[:].indirect(offs_sb[:]))
+
+        w1_bf = own([P, PACK * H], BF16, "w1_bf")
+        w1_bf_dealt = w1_bf[:].rearrange("p (t m j) -> p m t j", t=PACK, j=PACK)
+        for u in range(2):
+            nc.scalar.copy(out=w1_bf_dealt[:, u * P // 2 : (u + 1) * P // 2], in_=w1_raw[u][:].rearrange("p j (m t) -> p m t j", t=PACK))
+        w1_word = own([P, H], U32, "w1_word")
+        w1_scale = own([P, H], U8, "w1_scale")
+        nc.vector.quantize_mx(out=w1_word[:].bitcast(FP8X4), scales=w1_scale[:], in_=w1_bf[:])
+
+        x_word = own([P, S], U32, "x_word")
+        for a in (0, HALF):
+            nc.vector.tensor_copy(out=x_word[:, a : a + HALF], in_=x_word_table[:].indirect(entries(offs_sb, a, a + HALF)))
+        w2_scale = own([P, H], U8, "w2_scale")
+        nc.vector.tensor_copy(
+            out=w2_scale[:].rearrange("p (t m) -> p t m", t=PACK),
+            in_=w2_scale_raw[:].rearrange("p (m t) -> p t m", t=PACK),
         )
 
-        xs = sb([P, S], U8, "xs")
-        nc.vector.tensor_copy(out=xs[:], in_=xs_all[:].indirect(offs_sb[:]))
-        w1_bf = sb([P, 4 * H], BF16, "w1_bf")
-        w1_bf_v = w1_bf[:].rearrange("p (t m j) -> p m t j", t=4, j=4)
-        nc.scalar.copy(out=w1_bf_v[:, 0:64], in_=w1_raw[0][:].rearrange("p j (m t) -> p m t j", t=4))
-        nc.vector.tensor_copy(out=w1_bf_v[:, 64:128], in_=w1_raw[1][:].rearrange("p j (m t) -> p m t j", t=4))
-        w1c = sb([P, H], U32, "w1c")
-        w1s = sb([P, H], U8, "w1s")
-        nc.vector.quantize_mx(out=w1c[:].bitcast(FP8X4), scales=w1s[:], in_=w1_bf[:])
-
-        xw = sb([P, S], U32, "xw")
-        for u in range(2):
-            nc.vector.tensor_copy(out=xw[:, 256 * u : 256 * (u + 1)], in_=xw_all[:].indirect(offs_sb[:, 16 * u : 16 * (u + 1)]))
-        w2s = sb([P, H], U8, "w2s")
-        nc.vector.tensor_copy(out=w2s[:].rearrange("p (t m) -> p t m", t=4), in_=w2s_raw[:].rearrange("p (m t) -> p t m", t=4))
-
-        y = [sb([P, S], F32, "y%d" % t) for t in range(4)]
-        pieces = [(0, 0, 256), (0, 256, 512)] + [(t, 0, 512) for t in range(1, 4)]
-        for t, a, b in pieces:
-            acc = psum.tile([P, S], F32, name="acc", tag="mm", bufs=4)
+        for t, a, b in [(0, 0, HALF), (0, HALF, S)] + [(t, 0, S) for t in range(1, PACK)]:
+            y_bank = product_bank([P, S], "y_bank")
             nc.tensor.matmul_mx(
-                out=acc[:, 0 : b - a],
-                lhsT=w1c[:, P * t : P * (t + 1)].bitcast(FP8X4),
-                lhsT_scale=w1s[:, P * t : P * (t + 1)],
-                rhs=xw[:, a:b].bitcast(FP8X4),
-                rhs_scale=xs[:, a:b],
+                out=y_bank[:, 0 : b - a],
+                lhsT=w1_word[:, P * t : P * (t + 1)].bitcast(FP8X4),
+                lhsT_scale=w1_scale[:, P * t : P * (t + 1)],
+                rhs=x_word[:, a:b].bitcast(FP8X4),
+                rhs_scale=x_scale[:, a:b],
                 start=True,
                 stop=True,
             )
-            nc.scalar.copy(out=y[t][:, a:b], in_=acc[:, 0 : b - a])
+            nc.scalar.copy(out=y[t][:, a:b], in_=y_bank[:, 0 : b - a])
 
-        h = [sb([P, S], F32, "h%d" % t) for t in range(4)]
-        starts = [sum(CHUNKS[:c]) for c in range(len(CHUNKS))]
-        LATE = PE_TILES - 1
-        h2 = [sb([P, S], F32, "h2_%d" % t) if t < LATE else None for t in range(4)]
-        late = [turns.tile([P, n], F32, name="late%d" % c, offset=2048 * (c + 1), align_bytes=64) for c, n in enumerate(CHUNKS)]
+        last_turned = TURNED - 1
+        sum_place = (len(PIECES) + 1) * REGION
+        h = [own([P, S], F32, "h%d" % t) for t in range(PACK)]
+        h_copy = [None] * PACK
+        h_last = [placed([P, b - a], F32, "h_last%d" % g, (g + 1) * REGION) for g, (a, b) in enumerate(PIECES)]
 
-        def hop1(dst, t, lst, u):
-            cols = slice(256 * u, 256 * (u + 1))
-            nc.vector.tensor_tensor(dst[:, cols], y[t][:].indirect(lst[:, 16 * u : 16 * (u + 1)]), ga_sb[:, cols], ALU.mult)
+        def weighted_neighbours(dst, t, list_tile, a, b):
+            nc.vector.tensor_tensor(dst[:, a:b], y[t][:].indirect(entries(list_tile, a, b)), ga_sb[:, a:b], ALU.mult)
 
-        for t in range(4):
-            m1 = sb([P, S], F32, "m1_%d" % t)
-            m2 = sb([P, S], F32, "m2_%d" % t)
-            if t < PE_TILES:
-                for u in range(2):
-                    hop1(m1, t, p1_sb, u)
-                for u in range(2):
-                    hop1(m2, t, p2_sb, u)
-                ht = psum.tile([P, 4, P], F32, name="ht", tag="ht", bufs=2)
-                for n, term in enumerate((y[t], m1, m2)):
-                    for b in range(4):
-                        nc.tensor.matmul(ht[:, b, :], term[:, P * b : P * (b + 1)], ident[:], is_transpose=True, start=(n == 0 and b == 0), stop=(n == 2 and b == 3))
-                ht_sb = keep.tile([P, 4, P], F32, name="ht_sb%d" % t, tag="ht_sb%d" % t, align_bytes=64)
-                nc.scalar.copy(out=ht_sb[:], in_=ht[:])
-                hb = psum.tile([P, 4, P], F32, name="hb", tag="hb", bufs=2)
-                for b in range(4):
-                    nc.tensor.transpose(hb[:, b, :], ht_sb[:, b, :], ident[:])
-                nc.scalar.copy(out=h[t][:], in_=hb[:].rearrange("p b j -> p (b j)"))
-                if t == LATE:
-                    for c, n in enumerate(CHUNKS):
-                        nc.scalar.copy(out=late[c][:], in_=hb[:].rearrange("p b j -> p (b j)")[:, starts[c] : starts[c] + n])
+        for t in range(PACK):
+            n1 = own([P, S], F32, "n1_%d" % t)
+            n2 = own([P, S], F32, "n2_%d" % t)
+            weighted_neighbours(n1, t, p1_sb, 0, S)
+            if t < TURNED:
+                weighted_neighbours(n2, t, p2_sb, 0, S)
+                sum_bank = psum.tile([P, PACK, P], F32, name="sum_bank")
+                for n, term in enumerate((y[t], n1, n2)):
+                    for b in range(S // P):
+                        nc.tensor.matmul(
+                            sum_bank[:, b, :],
+                            term[:, P * b : P * (b + 1)],
+                            identity[:],
+                            is_transpose=True,
+                            start=(n == 0 and b == 0),
+                            stop=(n == 2 and b == S // P - 1),
+                        )
+                if t == last_turned:
+                    turned = placed([P, PACK, P], F32, "turned%d" % t, sum_place + REGION // 4)
                 else:
-                    nc.scalar.copy(out=h2[t][:], in_=hb[:].rearrange("p b j -> p (b j)"))
+                    turned = own([P, PACK, P], F32, "turned%d" % t)
+                nc.scalar.copy(out=turned[:], in_=sum_bank[:])
+                back_bank = psum.tile([P, S], F32, name="back_bank")
+                for b in range(S // P):
+                    nc.tensor.transpose(back_bank[:, P * b : P * (b + 1)], turned[:, b, :], identity[:])
+                nc.scalar.copy(out=h[t][:], in_=back_bank[:])
+                if t == last_turned:
+                    last_bank = back_bank
+                    nc.scalar.copy(out=h_last[0][:], in_=last_bank[:, PIECES[0][0] : PIECES[0][1]])
+                else:
+                    h_copy[t] = own([P, S], F32, "h_copy%d" % t)
+                    nc.scalar.copy(out=h_copy[t][:], in_=back_bank[:])
             else:
-                part = sb([P, S], F32, "part%d" % t)
-                h2[t] = keep.tile([P, S], F32, name="h2_%d" % t, tag="ht_sb%d" % LATE, align_bytes=64)
-                hop1(m1, t, p1_sb, 0)
-                hop1(m1, t, p1_sb, 1)
-                hop1(m2, t, p2_sb, 0)
-                nc.vector.tensor_tensor(part[:], m1[:], y[t][:], ALU.add)
-                hop1(m2, t, p2_sb, 1)
-                for u in range(2):
-                    cols = slice(256 * u, 256 * (u + 1))
-                    nc.vector.tensor_tensor(h[t][:, cols], part[:, cols], m2[:, cols], ALU.add)
-                    nc.scalar.copy(out=h2[t][:, cols], in_=h[t][:, cols])
+                part = own([P, S], F32, "part%d" % t)
+                h_copy[t] = placed([P, S], F32, "h_copy%d" % t, sum_place + (t % 2) * REGION // 2)
+                weighted_neighbours(n2, t, p2_sb, 0, HALF)
+                nc.vector.tensor_tensor(part[:], n1[:], y[t][:, 0:S], ALU.add)
+                weighted_neighbours(n2, t, p2_sb, HALF, S)
+                for a in (0, HALF):
+                    nc.vector.tensor_tensor(h[t][:, a : a + HALF], part[:, a : a + HALF], n2[:, a : a + HALF], ALU.add)
+                    nc.scalar.copy(out=h_copy[t][:, a : a + HALF], in_=h[t][:, a : a + HALF])
+        for g in range(1, len(PIECES)):
+            nc.scalar.copy(out=h_last[g][:], in_=last_bank[:, PIECES[g][0] : PIECES[g][1]])
 
-        oc = sb([P, S], U32, "oc")
-        osc = sb([P, S], U8, "osc")
-        out0_v = out_0.rearrange("(p t) j -> p t j", t=4)
-        out1_v = out_1[0].rearrange("p c r -> p (c r)").bitcast(I32)
+        out_word = own([P, S], U32, "out_word")
+        out_scale = own([P, S], U8, "out_scale")
+        out_rows = out_0.rearrange("(p t) j -> p t j", t=PACK)
+        out_word_hbm = out_1[0].rearrange("p c r -> p (c r)").bitcast(I32)
+        z = [None] * CHUNKS
+        result = [None] * CHUNKS
 
-        zc = [None] * len(CHUNKS)
-        zs = [None] * len(CHUNKS)
-        z = [None] * len(CHUNKS)
-        o_sb = [None] * len(CHUNKS)
-        ob = [None] * len(CHUNKS)
+        def side_by_side(tile):
+            return tile[:].rearrange("p (g i t) -> p g t i", i=4, t=PACK)
 
-        def hop2(c):
-            a, n = starts[c], CHUNKS[c]
-            nd = turns.tile([P, 4, n], F32, name="nd%d" % c, offset=2048 * c, align_bytes=64)
-            for t in [u for u in range(4) if u != LATE] + [LATE]:
-                own = late[c][:] if t == LATE else h2[t][:, a : a + n]
-                nc.vector.tensor_tensor(nd[:, t, :], h[t][:].indirect(q1_sb[:, a // 16 : (a + n) // 16]), own, ALU.subtract)
-            z[c] = turns.tile([P, 4 * n], BF16, name="z%d" % c, offset=2048 * (c + 2) + 512, align_bytes=64)
-            nc.scalar.activation(
-                out=z[c][:].rearrange("p (g i t) -> p g t i", i=4, t=4),
-                in_=nd[:].rearrange("p t (g i) -> p g t i", i=4),
-                func=ACT.Gelu_apprx_tanh,
-                scale=-1.0,
-            )
+        def by_planes(planes):
+            return planes.rearrange("p t (g i) -> p g t i", i=4)
 
-        def product(c):
-            a, n = starts[c], CHUNKS[c]
-            zc = sb([P, n], U32, "zc%d" % c)
-            zs = sb([P, n], U8, "zs%d" % c)
-            nc.vector.quantize_mx(out=zc[:].bitcast(FP8X4), scales=zs[:], in_=z[c][:])
-            o_sb[c] = sb([P, 4, n], F32, "o_sb%d" % c)
-            ob[c] = sb([P, 4 * n], BF16, "ob%d" % c)
-            per = 2 if c == len(CHUNKS) - 1 else S // n
-            for g in range(4 // per):
-                acc = psum.tile([P, per, n], F32, name="acc2", tag="mm", bufs=4)
-                for k in range(per):
-                    t = per * g + k
+        def second_hop(g):
+            a, b = PIECES[g]
+            minus_d = placed([P, PACK, b - a], F32, "minus_d%d" % g, g * REGION)
+            for t in [t for t in range(PACK) if t != last_turned] + [last_turned]:
+                own_values = h_last[g][:] if t == last_turned else h_copy[t][:, a:b]
+                nc.vector.tensor_tensor(minus_d[:, t, :], h[t][:].indirect(entries(q1_sb, a, b)), own_values, ALU.subtract)
+            for c in range(a // CHUNK, b // CHUNK):
+                if g == 0:
+                    z[c] = placed([P, PACK * CHUNK], BF16, "z%d" % c, 2 * REGION + CHUNK * 4 + c * PACK * CHUNK * 2)
+                else:
+                    z[c] = own([P, PACK * CHUNK], BF16, "z%d" % c)
+                cols = slice(c * CHUNK - a, (c + 1) * CHUNK - a)
+                nc.scalar.activation(out=side_by_side(z[c]), in_=by_planes(minus_d[:, :, cols]), func=GELU, scale=-1.0, bias=zero[:, 1:2])
+
+        def second_product(c):
+            z_word = own([P, CHUNK], U32, "z_word%d" % c)
+            z_scale = own([P, CHUNK], U8, "z_scale%d" % c)
+            nc.vector.quantize_mx(out=z_word[:].bitcast(FP8X4), scales=z_scale[:], in_=z[c][:])
+            result[c] = own([P, PACK, CHUNK], F32, "result%d" % c)
+            banks = 2 if c == CHUNKS - 1 else 1
+            per_bank = PACK // banks
+            for k in range(banks):
+                out_bank = product_bank([P, per_bank, CHUNK], "out_bank")
+                for t in range(per_bank * k, per_bank * (k + 1)):
                     nc.tensor.matmul_mx(
-                        out=acc[:, k, :],
-                        lhsT=w2w[:, 2 * P * t : 2 * P * (t + 1)].bitcast(FP4X4),
-                        lhsT_scale=w2s[:, P * t : P * (t + 1)],
-                        rhs=zc[:].bitcast(FP8X4),
-                        rhs_scale=zs[:],
+                        out=out_bank[:, t - per_bank * k, :],
+                        lhsT=w2_word[:, 2 * P * t : 2 * P * (t + 1)].bitcast(FP4X4),
+                        lhsT_scale=w2_scale[:, P * t : P * (t + 1)],
+                        rhs=z_word[:].bitcast(FP8X4),
+                        rhs_scale=z_scale[:],
                         start=True,
                         stop=True,
                     )
-                if c == len(CHUNKS) - 1 and g == 1:
-                    nc.vector.tensor_copy(out=o_sb[c][:, per * g : per * (g + 1), :], in_=acc[:])
+                planes = result[c][:, per_bank * k : per_bank * (k + 1), :]
+                if k == 0:
+                    nc.scalar.copy(out=planes, in_=out_bank[:])
                 else:
-                    nc.scalar.copy(out=o_sb[c][:, per * g : per * (g + 1), :], in_=acc[:])
-            nc.sync.dma_start(out=out0_v[:, :, a : a + n], in_=o_sb[c][:])
+                    nc.vector.tensor_copy(out=planes, in_=out_bank[:])
+            nc.sync.dma_start(out=out_rows[:, :, c * CHUNK : (c + 1) * CHUNK], in_=result[c][:])
 
-        def planes(c):
-            a, n = starts[c], CHUNKS[c]
-            dst = ob[c][:].rearrange("p (g i t) -> p g t i", i=4, t=4)
-            src = o_sb[c][:].rearrange("p t (g i) -> p g t i", i=4)
-            if c in CAST_ON_SCALAR:
-                nc.scalar.copy(out=dst, in_=src)
-            else:
-                nc.vector.tensor_copy(out=dst, in_=src)
-            nc.vector.quantize_mx(out=oc[:, a : a + n].bitcast(FP8X4), scales=osc[:, a : a + n], in_=ob[c][:])
-            if c >= len(CHUNKS) - 2:
-                a0 = a if c == len(CHUNKS) - 1 else 0
-                nc.sync.dma_start(out=out1_v[:, a0 : a + n], in_=oc[:, a0 : a + n].bitcast(I32))
+        def quantise_result(c):
+            cols = slice(c * CHUNK, (c + 1) * CHUNK)
+            rounded = own([P, PACK * CHUNK], BF16, "rounded%d" % c)
+            nc.vector.tensor_copy(out=side_by_side(rounded), in_=by_planes(result[c][:]))
+            nc.vector.quantize_mx(out=out_word[:, cols].bitcast(FP8X4), scales=out_scale[:, cols], in_=rounded[:])
 
-        last = len(CHUNKS)
-        for c in range(last + 1):
-            if c < last:
-                hop2(c)
-            if 1 <= c <= last:
-                product(c - 1)
-        for c in range(last):
-            planes(c)
-        for q in range(4):
-            eng = nc.sync if q % 2 == 0 else nc.scalar
-            eng.dma_start(out=out_2[0][4 * q : 4 * q + 4, :].bitcast(I32), in_=osc[32 * q : 32 * q + 4, :].bitcast(I32))
+        for g in range(len(PIECES) + 1):
+            if g < len(PIECES):
+                second_hop(g)
+            if g > 0:
+                for c in range(PIECES[g - 1][0] // CHUNK, PIECES[g - 1][1] // CHUNK):
+                    second_product(c)
+        for first, end in ((0, CHUNKS - 1), (CHUNKS - 1, CHUNKS)):
+            for c in range(first, end):
+                quantise_result(c)
+            cols = slice(first * CHUNK, end * CHUNK)
+            nc.sync.dma_start(out=out_word_hbm[:, cols], in_=out_word[:, cols].bitcast(I32))
+        for q in range(PACK):
+            queue = nc.sync if q % 2 == 0 else nc.scalar
+            queue.dma_start(out=out_2[0][PACK * q : PACK * (q + 1), :].bitcast(I32), in_=scale_rows(out_scale, q))

@@ -27,6 +27,7 @@ CHUNKS = S // CHUNK
 FLOPS = 2 * H * H * S * 2
 
 TURNED = 3
+W1_CUT = 320
 PIECES = ((0, 2 * CHUNK), (2 * CHUNK, 3 * CHUNK), (3 * CHUNK, 4 * CHUNK))
 REGION = PACK * 2 * CHUNK * 4
 
@@ -63,7 +64,8 @@ def tile_picked_twohop8_gelu_po_kernel(
         x_word_table = own([P, T], U32, "x_word_table")
         w2_scale_raw = own([P, H], U8, "w2_scale_raw")
         w2_word_raw = own([P, 2 * H], U8, "w2_word_raw")
-        w1_raw = [own([P, PACK, H // 2], F32, "w1_raw%d" % u) for u in range(2)]
+        w1_first = own([P, PACK, W1_CUT], F32, "w1_first")
+        w1_second = own([P, PACK, H - W1_CUT], F32, "w1_second")
         ga_sb = own([P, S], F32, "ga_sb")
 
         nc.gpsimd.memset(x_scale_table[:].bitcast(I32), 0)
@@ -74,8 +76,8 @@ def tile_picked_twohop8_gelu_po_kernel(
         nc.sync.dma_start(out=w2_word_raw[:].bitcast(I32), in_=w2_words[0].bitcast(I32))
         nc.sync.dma_start(p2_sb[:], p2)
         nc.sync.dma_start(q1_sb[:], q1)
-        for u in range(2):
-            nc.sync.dma_start(out=w1_raw[u][:], in_=w1_rows[:, :, u * H // 2 : (u + 1) * H // 2])
+        nc.sync.dma_start(out=w1_first[:], in_=w1_rows[:, :, 0:W1_CUT])
+        nc.sync.dma_start(out=w1_second[:], in_=w1_rows[:, :, W1_CUT:H])
         nc.sync.dma_start(out=x_word_table[:].bitcast(I32), in_=x_words[0].rearrange("p c r -> p (c r)").bitcast(I32))
         for q in range(PACK):
             nc.scalar.dma_start(out=scale_rows(x_scale_table, q), in_=x_scales[0][PACK * q : PACK * (q + 1), :].bitcast(I32))
@@ -100,13 +102,13 @@ def tile_picked_twohop8_gelu_po_kernel(
             out=w2_word[:].rearrange("p (t m b) -> p t m b", t=PACK, b=2),
             in_=w2_word_raw[:].rearrange("p (m t b) -> p t m b", t=PACK, b=2),
         )
-        x_scale = own([P, S], U8, "x_scale")
-        nc.vector.tensor_copy(out=x_scale[:], in_=x_scale_table[:].indirect(offs_sb[:]))
 
         w1_bf = own([P, PACK * H], BF16, "w1_bf")
         w1_bf_dealt = w1_bf[:].rearrange("p (t m j) -> p m t j", t=PACK, j=PACK)
-        for u in range(2):
-            nc.scalar.copy(out=w1_bf_dealt[:, u * P // 2 : (u + 1) * P // 2], in_=w1_raw[u][:].rearrange("p j (m t) -> p m t j", t=PACK))
+        nc.vector.tensor_copy(out=w1_bf_dealt[:, 0 : W1_CUT // PACK], in_=w1_first[:].rearrange("p j (m t) -> p m t j", t=PACK))
+        nc.scalar.copy(out=w1_bf_dealt[:, W1_CUT // PACK : P], in_=w1_second[:].rearrange("p j (m t) -> p m t j", t=PACK))
+        x_scale = own([P, S], U8, "x_scale")
+        nc.vector.tensor_copy(out=x_scale[:], in_=x_scale_table[:].indirect(offs_sb[:]))
         w1_word = own([P, H], U32, "w1_word")
         w1_scale = own([P, H], U8, "w1_scale")
         nc.vector.quantize_mx(out=w1_word[:].bitcast(FP8X4), scales=w1_scale[:], in_=w1_bf[:])

@@ -75,8 +75,8 @@ def tile_picked_twohop8_gelu_po_kernel(
         nc.sync.dma_start(p1_sb[:], p1)
         nc.sync.dma_start(out=w2_word_raw[:].bitcast(I32), in_=w2_words[0].bitcast(I32))
         nc.sync.dma_start(p2_sb[:], p2)
-        nc.sync.dma_start(q1_sb[:], q1)
         nc.sync.dma_start(out=w1_first[:], in_=w1_rows[:, :, 0:W1_CUT])
+        nc.sync.dma_start(q1_sb[:], q1)
         nc.sync.dma_start(out=w1_second[:], in_=w1_rows[:, :, W1_CUT:H])
         nc.sync.dma_start(out=x_word_table[:].bitcast(I32), in_=x_words[0].rearrange("p c r -> p (c r)").bitcast(I32))
         for q in range(PACK):
@@ -195,11 +195,11 @@ def tile_picked_twohop8_gelu_po_kernel(
         z = [None] * CHUNKS
         result = [None] * CHUNKS
 
-        def side_by_side(tile):
-            return tile[:].rearrange("p (g i t) -> p g t i", i=4, t=PACK)
+        def side_by_side(pairs):
+            return pairs.rearrange("p (j t) -> p j t", t=PACK)
 
         def by_planes(planes):
-            return planes.rearrange("p t (g i) -> p g t i", i=4)
+            return planes.rearrange("p t j -> p j t")
 
         def second_hop(g):
             a, b = PIECES[g]
@@ -213,7 +213,7 @@ def tile_picked_twohop8_gelu_po_kernel(
                 else:
                     z[c] = own([P, PACK * CHUNK], BF16, "z%d" % c)
                 cols = slice(c * CHUNK - a, (c + 1) * CHUNK - a)
-                nc.scalar.activation(out=side_by_side(z[c]), in_=by_planes(minus_d[:, :, cols]), func=GELU, scale=-1.0, bias=zero[:, 1:2])
+                nc.scalar.activation(out=side_by_side(z[c][:]), in_=by_planes(minus_d[:, :, cols]), func=GELU, scale=-1.0, bias=zero[:, 1:2])
 
         def second_product(c):
             z_word = own([P, CHUNK], U32, "z_word%d" % c)
@@ -234,18 +234,16 @@ def tile_picked_twohop8_gelu_po_kernel(
                         start=True,
                         stop=True,
                     )
-                planes = result[c][:, per_bank * k : per_bank * (k + 1), :]
-                if k == 0:
-                    nc.scalar.copy(out=planes, in_=out_bank[:])
-                else:
-                    nc.vector.tensor_copy(out=planes, in_=out_bank[:])
+                nc.scalar.copy(out=result[c][:, per_bank * k : per_bank * (k + 1), :], in_=out_bank[:])
             nc.sync.dma_start(out=out_rows[:, :, c * CHUNK : (c + 1) * CHUNK], in_=result[c][:])
 
-        def quantise_result(c):
-            cols = slice(c * CHUNK, (c + 1) * CHUNK)
-            rounded = own([P, PACK * CHUNK], BF16, "rounded%d" % c)
-            nc.vector.tensor_copy(out=side_by_side(rounded), in_=by_planes(result[c][:]))
-            nc.vector.quantize_mx(out=out_word[:, cols].bitcast(FP8X4), scales=out_scale[:, cols], in_=rounded[:])
+        def quantise_result(g):
+            a, b = PIECES[g]
+            rounded = own([P, PACK * (b - a)], BF16, "rounded%d" % g)
+            for c in range(a // CHUNK, b // CHUNK):
+                first = PACK * (c * CHUNK - a)
+                nc.vector.tensor_copy(out=side_by_side(rounded[:, first : first + PACK * CHUNK]), in_=by_planes(result[c][:]))
+            nc.vector.quantize_mx(out=out_word[:, a:b].bitcast(FP8X4), scales=out_scale[:, a:b], in_=rounded[:])
 
         for g in range(len(PIECES) + 1):
             if g < len(PIECES):
@@ -253,10 +251,10 @@ def tile_picked_twohop8_gelu_po_kernel(
             if g > 0:
                 for c in range(PIECES[g - 1][0] // CHUNK, PIECES[g - 1][1] // CHUNK):
                     second_product(c)
-        for first, end in ((0, CHUNKS - 1), (CHUNKS - 1, CHUNKS)):
-            for c in range(first, end):
-                quantise_result(c)
-            cols = slice(first * CHUNK, end * CHUNK)
+        for first, end in ((0, len(PIECES) - 1), (len(PIECES) - 1, len(PIECES))):
+            for g in range(first, end):
+                quantise_result(g)
+            cols = slice(PIECES[first][0], PIECES[end - 1][1])
             nc.sync.dma_start(out=out_word_hbm[:, cols], in_=out_word[:, cols].bitcast(I32))
         for q in range(PACK):
             queue = nc.sync if q % 2 == 0 else nc.scalar

@@ -64,27 +64,28 @@ def tile_picked_twohop8_gelu_po_kernel(
         x_word_table = own([P, T], U32, "x_word_table")
         w2_scale_raw = own([P, H], U8, "w2_scale_raw")
         w2_word_raw = own([P, 2 * H], U8, "w2_word_raw")
-        w1_first = own([P, PACK, W1_CUT], F32, "w1_first")
-        w1_second = own([P, PACK, H - W1_CUT], F32, "w1_second")
+        w1_raw = own([P, PACK, H], F32, "w1_raw")
         ga_sb = own([P, S], F32, "ga_sb")
 
-        nc.gpsimd.memset(x_scale_table[:].bitcast(I32), 0)
-        nc.gpsimd.memset(w2_scale_raw[:].bitcast(I32), 0)
+        def scale_rows_apart(tile, r):
+            return tile[r:P:QUADRANT, :].bitcast(I32)
+
+        nc.vector.memset(x_scale_table[:].bitcast(I32), 0)
+        nc.vector.memset(w2_scale_raw[:].bitcast(I32), 0)
         w1_rows = w1.rearrange("(p j) c -> p j c", j=PACK)
+        nc.sync.dma_start(out=w1_raw[:, 0:1, :], in_=w1_rows[:, 0:1, :])
+        for r in range(PACK):
+            nc.sync.dma_start(out=scale_rows_apart(x_scale_table, r), in_=x_scales[0][r : PACK * PACK : PACK, :].bitcast(I32))
         nc.sync.dma_start(offs_sb[:], offs)
+        nc.sync.dma_start(out=w1_raw[:, 1:PACK, :], in_=w1_rows[:, 1:PACK, :])
+        nc.sync.dma_start(out=x_word_table[:].bitcast(I32), in_=x_words[0].rearrange("p c r -> p (c r)").bitcast(I32))
         nc.sync.dma_start(p1_sb[:], p1)
         nc.sync.dma_start(out=w2_word_raw[:].bitcast(I32), in_=w2_words[0].bitcast(I32))
-        nc.sync.dma_start(p2_sb[:], p2)
-        nc.sync.dma_start(out=w1_first[:], in_=w1_rows[:, :, 0:W1_CUT])
-        nc.sync.dma_start(q1_sb[:], q1)
-        nc.sync.dma_start(out=w1_second[:], in_=w1_rows[:, :, W1_CUT:H])
-        nc.sync.dma_start(out=x_word_table[:].bitcast(I32), in_=x_words[0].rearrange("p c r -> p (c r)").bitcast(I32))
-        for q in range(PACK):
-            nc.scalar.dma_start(out=scale_rows(x_scale_table, q), in_=x_scales[0][PACK * q : PACK * (q + 1), :].bitcast(I32))
+        for r in range(PACK):
+            nc.sync.dma_start(out=scale_rows_apart(w2_scale_raw, r), in_=w2_scales[0][r : PACK * PACK : PACK, :].bitcast(I32))
         nc.sync.dma_start(out=ga_sb[:], in_=ga)
-        for q in range(PACK):
-            queue = nc.sync if q < PACK // 2 else nc.gpsimd
-            queue.dma_start(out=scale_rows(w2_scale_raw, q), in_=w2_scales[0][PACK * q : PACK * (q + 1), :].bitcast(I32))
+        nc.sync.dma_start(p2_sb[:], p2)
+        nc.sync.dma_start(q1_sb[:], q1)
 
         zero = own([P, 2], F32, "zero")
         nc.vector.memset(zero[:, 0:1], 0.0)
@@ -97,18 +98,13 @@ def tile_picked_twohop8_gelu_po_kernel(
         for t in range(PACK):
             nc.vector.memset(y[t][:, S : 2 * S], 0.0)
 
-        w2_word = own([P, 2 * H], U8, "w2_word")
-        nc.vector.tensor_copy(
-            out=w2_word[:].rearrange("p (t m b) -> p t m b", t=PACK, b=2),
-            in_=w2_word_raw[:].rearrange("p (m t b) -> p t m b", t=PACK, b=2),
-        )
-
         w1_bf = own([P, PACK * H], BF16, "w1_bf")
         w1_bf_dealt = w1_bf[:].rearrange("p (t m j) -> p m t j", t=PACK, j=PACK)
-        nc.vector.tensor_copy(out=w1_bf_dealt[:, 0 : W1_CUT // PACK], in_=w1_first[:].rearrange("p j (m t) -> p m t j", t=PACK))
-        nc.scalar.copy(out=w1_bf_dealt[:, W1_CUT // PACK : P], in_=w1_second[:].rearrange("p j (m t) -> p m t j", t=PACK))
         x_scale = own([P, S], U8, "x_scale")
         nc.vector.tensor_copy(out=x_scale[:], in_=x_scale_table[:].indirect(offs_sb[:]))
+        w1_by_column = w1_raw[:].rearrange("p j (m t) -> p m t j", t=PACK)
+        nc.vector.tensor_copy(out=w1_bf_dealt[:, 0 : W1_CUT // PACK], in_=w1_by_column[:, 0 : W1_CUT // PACK])
+        nc.scalar.copy(out=w1_bf_dealt[:, W1_CUT // PACK : P], in_=w1_by_column[:, W1_CUT // PACK : P])
         w1_word = own([P, H], U32, "w1_word")
         w1_scale = own([P, H], U8, "w1_scale")
         nc.vector.quantize_mx(out=w1_word[:].bitcast(FP8X4), scales=w1_scale[:], in_=w1_bf[:])
@@ -116,6 +112,11 @@ def tile_picked_twohop8_gelu_po_kernel(
         x_word = own([P, S], U32, "x_word")
         for a in (0, HALF):
             nc.vector.tensor_copy(out=x_word[:, a : a + HALF], in_=x_word_table[:].indirect(entries(offs_sb, a, a + HALF)))
+        w2_word = own([P, 2 * H], U8, "w2_word")
+        nc.vector.tensor_copy(
+            out=w2_word[:].rearrange("p (t m b) -> p t m b", t=PACK, b=2),
+            in_=w2_word_raw[:].rearrange("p (m t b) -> p t m b", t=PACK, b=2),
+        )
         w2_scale = own([P, H], U8, "w2_scale")
         nc.vector.tensor_copy(
             out=w2_scale[:].rearrange("p (t m) -> p t m", t=PACK),

@@ -13,6 +13,7 @@ FP8X4 = mybir.dt.float8_e4m3fn_x4
 FP4X4 = mybir.dt.float4_e2m1fn_x4
 ALU = mybir.AluOpType
 GELU = mybir.ActivationFunctionType.Gelu_apprx_tanh
+IDENTITY = mybir.ActivationFunctionType.Identity
 
 P = 128
 PACK = 4
@@ -50,6 +51,9 @@ def tile_picked_twohop8_gelu_po_kernel(
         def product_bank(shape, name):
             return psum.tile(shape, F32, name=name, tag="product", bufs=4)
 
+        def turn_bank(shape, name):
+            return psum.tile(shape, F32, name=name, tag="turn", bufs=3)
+
         def scale_rows(tile, q):
             return tile[QUADRANT * q : QUADRANT * q + PACK, :].bitcast(I32)
 
@@ -80,11 +84,12 @@ def tile_picked_twohop8_gelu_po_kernel(
         nc.sync.dma_start(out=w1_raw[:, 1:PACK, :], in_=w1_rows[:, 1:PACK, :])
         nc.sync.dma_start(out=x_word_table[:].bitcast(I32), in_=x_words[0].rearrange("p c r -> p (c r)").bitcast(I32))
         nc.sync.dma_start(p1_sb[:], p1)
+        nc.sync.dma_start(p2_sb[:], p2)
         nc.sync.dma_start(out=w2_word_raw[:].bitcast(I32), in_=w2_words[0].bitcast(I32))
         for r in range(PACK):
-            nc.sync.dma_start(out=scale_rows_apart(w2_scale_raw, r), in_=w2_scales[0][r : PACK * PACK : PACK, :].bitcast(I32))
+            queue = nc.gpsimd if r == PACK - 1 else nc.sync
+            queue.dma_start(out=scale_rows_apart(w2_scale_raw, r), in_=w2_scales[0][r : PACK * PACK : PACK, :].bitcast(I32))
         nc.sync.dma_start(out=ga_sb[:], in_=ga)
-        nc.sync.dma_start(p2_sb[:], p2)
         nc.sync.dma_start(q1_sb[:], q1)
 
         zero = own([P, 2], F32, "zero")
@@ -114,8 +119,8 @@ def tile_picked_twohop8_gelu_po_kernel(
             nc.vector.tensor_copy(out=x_word[:, a : a + HALF], in_=x_word_table[:].indirect(entries(offs_sb, a, a + HALF)))
         w2_word = own([P, 2 * H], U8, "w2_word")
         nc.vector.tensor_copy(
-            out=w2_word[:].rearrange("p (t m b) -> p t m b", t=PACK, b=2),
-            in_=w2_word_raw[:].rearrange("p (m t b) -> p t m b", t=PACK, b=2),
+            out=w2_word[:].bitcast(U16).rearrange("p (t m) -> p t m", t=PACK),
+            in_=w2_word_raw[:].bitcast(U16).rearrange("p (m t) -> p t m", t=PACK),
         )
         w2_scale = own([P, H], U8, "w2_scale")
         nc.vector.tensor_copy(
@@ -140,7 +145,11 @@ def tile_picked_twohop8_gelu_po_kernel(
         sum_place = (len(PIECES) + 1) * REGION
         h = [own([P, S], F32, "h%d" % t) for t in range(PACK)]
         h_copy = [None] * PACK
-        h_last = [placed([P, b - a], F32, "h_last%d" % g, (g + 1) * REGION) for g, (a, b) in enumerate(PIECES)]
+        h_last = [own([P, b - a], F32, "h_last%d" % g) for g, (a, b) in enumerate(PIECES)]
+        no_bias = placed([P, 1], F32, "no_bias", REGION)
+        nc.vector.memset(no_bias[:], 0.0)
+        first_bias = placed([P, 1], F32, "first_bias", 2 * REGION)
+        nc.vector.memset(first_bias[:], 0.0)
 
         def weighted_neighbours(dst, t, list_tile, a, b):
             nc.vector.tensor_tensor(dst[:, a:b], y[t][:].indirect(entries(list_tile, a, b)), ga_sb[:, a:b], ALU.mult)
@@ -173,7 +182,7 @@ def tile_picked_twohop8_gelu_po_kernel(
                 nc.scalar.copy(out=h[t][:], in_=back_bank[:])
                 if t == last_turned:
                     last_bank = back_bank
-                    nc.scalar.copy(out=h_last[0][:], in_=last_bank[:, PIECES[0][0] : PIECES[0][1]])
+                    nc.scalar.activation(out=h_last[0][:], in_=last_bank[:, PIECES[0][0] : PIECES[0][1]], func=IDENTITY, bias=no_bias[:])
                 else:
                     h_copy[t] = own([P, S], F32, "h_copy%d" % t)
                     nc.scalar.copy(out=h_copy[t][:], in_=back_bank[:])
@@ -197,10 +206,10 @@ def tile_picked_twohop8_gelu_po_kernel(
         result = [None] * CHUNKS
 
         def side_by_side(pairs):
-            return pairs.rearrange("p (j t) -> p j t", t=PACK)
+            return pairs.rearrange("p (c i t) -> p c t i", i=PACK, t=PACK)
 
         def by_planes(planes):
-            return planes.rearrange("p t j -> p j t")
+            return planes.rearrange("p t (c i) -> p c t i", i=PACK)
 
         def second_hop(g):
             a, b = PIECES[g]
@@ -209,12 +218,9 @@ def tile_picked_twohop8_gelu_po_kernel(
                 own_values = h_last[g][:] if t == last_turned else h_copy[t][:, a:b]
                 nc.vector.tensor_tensor(minus_d[:, t, :], h[t][:].indirect(entries(q1_sb, a, b)), own_values, ALU.subtract)
             for c in range(a // CHUNK, b // CHUNK):
-                if g == 0:
-                    z[c] = placed([P, PACK * CHUNK], BF16, "z%d" % c, 2 * REGION + CHUNK * 4 + c * PACK * CHUNK * 2)
-                else:
-                    z[c] = own([P, PACK * CHUNK], BF16, "z%d" % c)
+                z[c] = own([P, PACK * CHUNK], BF16, "z%d" % c)
                 cols = slice(c * CHUNK - a, (c + 1) * CHUNK - a)
-                nc.scalar.activation(out=side_by_side(z[c][:]), in_=by_planes(minus_d[:, :, cols]), func=GELU, scale=-1.0, bias=zero[:, 1:2])
+                nc.scalar.activation(out=side_by_side(z[c][:]), in_=by_planes(minus_d[:, :, cols]), func=GELU, scale=-1.0, bias=first_bias[:] if c == 0 else zero[:, 1:2])
 
         def second_product(c):
             z_word = own([P, CHUNK], U32, "z_word%d" % c)

@@ -104,10 +104,10 @@ def tile_picked_twohop8_gelu_po_kernel(
             nc.vector.memset(y[t][:, S : 2 * S], 0.0)
 
         w1_bf = own([P, PACK * H], BF16, "w1_bf")
-        w1_bf_dealt = w1_bf[:].rearrange("p (t m j) -> p m t j", t=PACK, j=PACK)
+        w1_bf_dealt = w1_bf[:].rearrange("p (t m j) -> p m j t", t=PACK, j=PACK)
         x_scale = own([P, S], U8, "x_scale")
         nc.vector.tensor_copy(out=x_scale[:], in_=x_scale_table[:].indirect(offs_sb[:]))
-        w1_by_column = w1_raw[:].rearrange("p j (m t) -> p m t j", t=PACK)
+        w1_by_column = w1_raw[:].rearrange("p j (m t) -> p m j t", t=PACK)
         nc.vector.tensor_copy(out=w1_bf_dealt[:, 0 : W1_CUT // PACK], in_=w1_by_column[:, 0 : W1_CUT // PACK])
         nc.scalar.copy(out=w1_bf_dealt[:, W1_CUT // PACK : P], in_=w1_by_column[:, W1_CUT // PACK : P])
         w1_word = own([P, H], U32, "w1_word")
@@ -119,16 +119,16 @@ def tile_picked_twohop8_gelu_po_kernel(
             nc.vector.tensor_copy(out=x_word[:, a : a + HALF], in_=x_word_table[:].indirect(entries(offs_sb, a, a + HALF)))
         w2_word = own([P, 2 * H], U8, "w2_word")
         nc.vector.tensor_copy(
-            out=w2_word[:].bitcast(U16).rearrange("p (t m) -> p t m", t=PACK),
-            in_=w2_word_raw[:].bitcast(U16).rearrange("p (m t) -> p t m", t=PACK),
+            out=w2_word[:].bitcast(U16).rearrange("p (t m) -> p m t", t=PACK),
+            in_=w2_word_raw[:].bitcast(U16).rearrange("p (m t) -> p m t", t=PACK),
         )
         w2_scale = own([P, H], U8, "w2_scale")
         nc.vector.tensor_copy(
-            out=w2_scale[:].rearrange("p (t m) -> p t m", t=PACK),
-            in_=w2_scale_raw[:].rearrange("p (m t) -> p t m", t=PACK),
+            out=w2_scale[:].rearrange("p (t m) -> p m t", t=PACK),
+            in_=w2_scale_raw[:].rearrange("p (m t) -> p m t", t=PACK),
         )
 
-        for t, a, b in [(0, 0, HALF), (0, HALF, S)] + [(t, 0, S) for t in range(1, PACK)]:
+        for t, a, b in [(0, a, b) for a, b in PIECES] + [(t, 0, S) for t in range(1, PACK)]:
             y_bank = product_bank([P, S], "y_bank")
             nc.tensor.matmul_mx(
                 out=y_bank[:, 0 : b - a],

@@ -242,7 +242,8 @@ def tile_picked_twohop8_gelu_po_kernel(
                         stop=True,
                     )
                 nc.scalar.copy(out=result[c][:, per_bank * k : per_bank * (k + 1), :], in_=out_bank[:])
-            nc.sync.dma_start(out=out_rows[:, :, c * CHUNK : (c + 1) * CHUNK], in_=result[c][:])
+            queue = nc.scalar if c == CHUNKS - 1 else nc.sync
+            queue.dma_start(out=out_rows[:, :, c * CHUNK : (c + 1) * CHUNK], in_=result[c][:])
 
         def quantise_result(g):
             a, b = PIECES[g]

@@ -28,7 +28,6 @@ CHUNKS = S // CHUNK
 FLOPS = 2 * H * H * S * 2
 
 TURNED = 3
-W1_CUT = 320
 PIECES = ((0, 2 * CHUNK), (2 * CHUNK, 3 * CHUNK), (3 * CHUNK, 4 * CHUNK))
 REGION = PACK * 2 * CHUNK * 4
 
@@ -68,7 +67,7 @@ def tile_picked_twohop8_gelu_po_kernel(
         x_word_table = own([P, T], U32, "x_word_table")
         w2_scale_raw = own([P, H], U8, "w2_scale_raw")
         w2_word_raw = own([P, 2 * H], U8, "w2_word_raw")
-        w1_raw = own([P, PACK, H], F32, "w1_raw")
+        w1_raw = [own([P, 2, H], F32, "w1_raw%d" % u) for u in range(2)]
         ga_sb = own([P, S], F32, "ga_sb")
 
         def scale_rows_apart(tile, r):
@@ -77,12 +76,12 @@ def tile_picked_twohop8_gelu_po_kernel(
         nc.vector.memset(x_scale_table[:].bitcast(I32), 0)
         nc.vector.memset(w2_scale_raw[:].bitcast(I32), 0)
         w1_rows = w1.rearrange("(p j) c -> p j c", j=PACK)
-        nc.sync.dma_start(out=w1_raw[:, 0:1, :], in_=w1_rows[:, 0:1, :])
+        nc.sync.dma_start(out=w1_raw[0][:], in_=w1_rows[:, 0:2, :])
         for r in range(PACK):
             nc.sync.dma_start(out=scale_rows_apart(x_scale_table, r), in_=x_scales[0][r : PACK * PACK : PACK, :].bitcast(I32))
         nc.sync.dma_start(offs_sb[:], offs)
-        nc.sync.dma_start(out=w1_raw[:, 1:PACK, :], in_=w1_rows[:, 1:PACK, :])
         nc.sync.dma_start(out=x_word_table[:].bitcast(I32), in_=x_words[0].rearrange("p c r -> p (c r)").bitcast(I32))
+        nc.sync.dma_start(out=w1_raw[1][:], in_=w1_rows[:, 2:PACK, :])
         nc.sync.dma_start(p1_sb[:], p1)
         nc.sync.dma_start(p2_sb[:], p2)
         nc.sync.dma_start(out=w2_word_raw[:].bitcast(I32), in_=w2_words[0].bitcast(I32))
@@ -107,16 +106,24 @@ def tile_picked_twohop8_gelu_po_kernel(
         w1_bf_dealt = w1_bf[:].rearrange("p (t m j) -> p m j t", t=PACK, j=PACK)
         x_scale = own([P, S], U8, "x_scale")
         nc.vector.tensor_copy(out=x_scale[:], in_=x_scale_table[:].indirect(offs_sb[:]))
-        w1_by_column = w1_raw[:].rearrange("p j (m t) -> p m j t", t=PACK)
-        nc.vector.tensor_copy(out=w1_bf_dealt[:, 0 : W1_CUT // PACK], in_=w1_by_column[:, 0 : W1_CUT // PACK])
-        nc.scalar.copy(out=w1_bf_dealt[:, W1_CUT // PACK : P], in_=w1_by_column[:, W1_CUT // PACK : P])
+        by_column = [raw[:].rearrange("p j (m t) -> p m j t", t=PACK) for raw in w1_raw]
+        nc.vector.tensor_copy(out=w1_bf_dealt[:, :, 0:2], in_=by_column[0])
+        x_word = own([P, S], U32, "x_word")
+        nc.vector.tensor_copy(out=x_word[:], in_=x_word_table[:].indirect(offs_sb[:]))
         w1_word = own([P, H], U32, "w1_word")
         w1_scale = own([P, H], U8, "w1_scale")
-        nc.vector.quantize_mx(out=w1_word[:].bitcast(FP8X4), scales=w1_scale[:], in_=w1_bf[:])
 
-        x_word = own([P, S], U32, "x_word")
-        for a in (0, HALF):
-            nc.vector.tensor_copy(out=x_word[:, a : a + HALF], in_=x_word_table[:].indirect(entries(offs_sb, a, a + HALF)))
+        def quantise_w1(first, end):
+            a, b = P * first, P * end
+            nc.vector.quantize_mx(out=w1_word[:, a:b].bitcast(FP8X4), scales=w1_scale[:, a:b], in_=w1_bf[:, PACK * a : PACK * b])
+
+        for t in (0, 1):
+            nc.vector.tensor_copy(out=w1_bf_dealt[:, :, 2:PACK, t], in_=by_column[1][:, :, :, t])
+        nc.scalar.copy(out=w1_bf_dealt[:, :, 2:PACK, 2:PACK], in_=by_column[1][:, :, :, 2:PACK])
+        quantise_w1(0, 1)
+        quantise_w1(1, 2)
+        quantise_w1(2, PACK)
+
         w2_word = own([P, 2 * H], U8, "w2_word")
         nc.vector.tensor_copy(
             out=w2_word[:].bitcast(U16).rearrange("p (t m) -> p m t", t=PACK),
@@ -128,7 +135,7 @@ def tile_picked_twohop8_gelu_po_kernel(
             in_=w2_scale_raw[:].rearrange("p (m t) -> p m t", t=PACK),
         )
 
-        for t, a, b in [(0, a, b) for a, b in PIECES] + [(t, 0, S) for t in range(1, PACK)]:
+        for t, a, b in [(0, S - b, S - a) for a, b in PIECES[::-1]] + [(t, 0, S) for t in range(1, PACK)]:
             y_bank = product_bank([P, S], "y_bank")
             nc.tensor.matmul_mx(
                 out=y_bank[:, 0 : b - a],

@@ -1,7 +1,6 @@
 from contextlib import ExitStack
 
 import concourse.mybir as mybir
-from concourse.masks import make_identity
 
 F32 = mybir.dt.float32
 BF16 = mybir.dt.bfloat16
@@ -13,7 +12,7 @@ FP8X4 = mybir.dt.float8_e4m3fn_x4
 FP4X4 = mybir.dt.float4_e2m1fn_x4
 ALU = mybir.AluOpType
 GELU = mybir.ActivationFunctionType.Gelu_apprx_tanh
-IDENTITY = mybir.ActivationFunctionType.Identity
+COPY = mybir.ActivationFunctionType.Copy
 
 P = 128
 PACK = 4
@@ -21,15 +20,12 @@ T = 2048
 S = 512
 H = 512
 HALF = S // 2
+HALVES = ((0, HALF), (HALF, S))
 LANES = 16
 QUADRANT = 32
 CHUNK = 128
 CHUNKS = S // CHUNK
 FLOPS = 2 * H * H * S * 2
-
-TURNED = 3
-PIECES = ((0, 2 * CHUNK), (2 * CHUNK, 3 * CHUNK), (3 * CHUNK, 4 * CHUNK))
-REGION = PACK * 2 * CHUNK * 4
 
 
 def tile_picked_twohop8_gelu_po_kernel(
@@ -38,20 +34,13 @@ def tile_picked_twohop8_gelu_po_kernel(
     nc = tc.nc
     with ExitStack() as ctx:
         keep = ctx.enter_context(tc.tile_pool(name="keep", bufs=1))
-        shared = ctx.enter_context(tc.tile_pool(name="shared", bufs=1))
-        psum = ctx.enter_context(tc.psum_pool(name="psum", bufs=2))
+        psum = ctx.enter_context(tc.psum_pool(name="psum", bufs=8))
 
         def own(shape, dtype, name):
             return keep.tile(shape, dtype, name=name, align_bytes=64)
 
-        def placed(shape, dtype, name, offset):
-            return shared.tile(shape, dtype, name=name, offset=offset, align_bytes=64)
-
-        def product_bank(shape, name):
-            return psum.tile(shape, F32, name=name, tag="product", bufs=4)
-
-        def turn_bank(shape, name):
-            return psum.tile(shape, F32, name=name, tag="turn", bufs=3)
+        def bank(shape, name):
+            return psum.tile(shape, F32, name=name, tag="product")
 
         def scale_rows(tile, q):
             return tile[QUADRANT * q : QUADRANT * q + PACK, :].bitcast(I32)
@@ -95,13 +84,6 @@ def tile_picked_twohop8_gelu_po_kernel(
         nc.vector.memset(zero[:, 0:1], 0.0)
         nc.scalar.activation(out=zero[:, 1:2], in_=zero[:, 0:1], func=GELU)
 
-        identity = own([P, P], F32, "identity")
-        make_identity(nc, identity[:])
-
-        y = [own([P, 2 * S], F32, "y%d" % t) for t in range(PACK)]
-        for t in range(PACK):
-            nc.vector.memset(y[t][:, S : 2 * S], 0.0)
-
         w1_bf = own([P, PACK * H], BF16, "w1_bf")
         w1_bf_dealt = w1_bf[:].rearrange("p (t m j) -> p m j t", t=PACK, j=PACK)
         x_scale = own([P, S], U8, "x_scale")
@@ -135,10 +117,13 @@ def tile_picked_twohop8_gelu_po_kernel(
             in_=w2_scale_raw[:].rearrange("p (m t) -> p m t", t=PACK),
         )
 
-        for t, a, b in [(0, S - b, S - a) for a, b in PIECES[::-1]] + [(t, 0, S) for t in range(1, PACK)]:
-            y_bank = product_bank([P, S], "y_bank")
+        y = [own([P, S], F32, "y%d" % t) for t in range(PACK)]
+        h = [own([P, S], F32, "h%d" % t) for t in range(PACK)]
+
+        def first_product(t, a, b, copy):
+            y_bank = bank([P, b - a], "y_bank")
             nc.tensor.matmul_mx(
-                out=y_bank[:, 0 : b - a],
+                out=y_bank[:],
                 lhsT=w1_word[:, P * t : P * (t + 1)].bitcast(FP8X4),
                 lhsT_scale=w1_scale[:, P * t : P * (t + 1)],
                 rhs=x_word[:, a:b].bitcast(FP8X4),
@@ -146,70 +131,46 @@ def tile_picked_twohop8_gelu_po_kernel(
                 start=True,
                 stop=True,
             )
-            nc.scalar.copy(out=y[t][:, a:b], in_=y_bank[:, 0 : b - a])
+            copy(out=y[t][:, a:b], in_=y_bank[:])
 
-        last_turned = TURNED - 1
-        sum_place = (len(PIECES) + 1) * REGION
-        h = [own([P, S], F32, "h%d" % t) for t in range(PACK)]
-        h_copy = [None] * PACK
-        h_last = [own([P, b - a], F32, "h_last%d" % g) for g, (a, b) in enumerate(PIECES)]
-        no_bias = placed([P, 1], F32, "no_bias", REGION)
-        nc.vector.memset(no_bias[:], 0.0)
-        first_bias = placed([P, 1], F32, "first_bias", 2 * REGION)
-        nc.vector.memset(first_bias[:], 0.0)
-
-        def weighted_neighbours(dst, t, list_tile, a, b):
-            nc.vector.tensor_tensor(dst[:, a:b], y[t][:].indirect(entries(list_tile, a, b)), ga_sb[:, a:b], ALU.mult)
+        def scalar_gather(dst, window, list_tile, a, b):
+            nc.scalar.activation(out=dst[:, a:b], in_=window[:].indirect(entries(list_tile, a, b)), func=COPY)
 
         for t in range(PACK):
-            n1 = own([P, S], F32, "n1_%d" % t)
-            n2 = own([P, S], F32, "n2_%d" % t)
-            weighted_neighbours(n1, t, p1_sb, 0, S)
-            if t < TURNED:
-                weighted_neighbours(n2, t, p2_sb, 0, S)
-                sum_bank = psum.tile([P, PACK, P], F32, name="sum_bank")
-                for n, term in enumerate((y[t], n1, n2)):
-                    for b in range(S // P):
-                        nc.tensor.matmul(
-                            sum_bank[:, b, :],
-                            term[:, P * b : P * (b + 1)],
-                            identity[:],
-                            is_transpose=True,
-                            start=(n == 0 and b == 0),
-                            stop=(n == 2 and b == S // P - 1),
-                        )
-                if t == last_turned:
-                    turned = placed([P, PACK, P], F32, "turned%d" % t, sum_place + REGION // 4)
-                else:
-                    turned = own([P, PACK, P], F32, "turned%d" % t)
-                nc.scalar.copy(out=turned[:], in_=sum_bank[:])
-                back_bank = psum.tile([P, S], F32, name="back_bank")
-                for b in range(S // P):
-                    nc.tensor.transpose(back_bank[:, P * b : P * (b + 1)], turned[:, b, :], identity[:])
-                nc.scalar.copy(out=h[t][:], in_=back_bank[:])
-                if t == last_turned:
-                    last_bank = back_bank
-                    nc.scalar.activation(out=h_last[0][:], in_=last_bank[:, PIECES[0][0] : PIECES[0][1]], func=IDENTITY, bias=no_bias[:])
-                else:
-                    h_copy[t] = own([P, S], F32, "h_copy%d" % t)
-                    nc.scalar.copy(out=h_copy[t][:], in_=back_bank[:])
+            first = own([P, S], F32, "first%d" % t)
+            both = own([P, S], F32, "both%d" % t)
+            if t == 0:
+                first_product(t, 0, HALF, nc.scalar.copy)
+                first_product(t, HALF, S, nc.vector.tensor_copy)
+                scalar_gather(first, y[t], p1_sb, 0, HALF)
+                nc.vector.tensor_copy(out=first[:, HALF:S], in_=y[t][:].indirect(entries(p1_sb, HALF, S)))
             else:
-                part = own([P, S], F32, "part%d" % t)
-                h_copy[t] = placed([P, S], F32, "h_copy%d" % t, sum_place + (t % 2) * REGION // 2)
-                weighted_neighbours(n2, t, p2_sb, 0, HALF)
-                nc.vector.tensor_tensor(part[:], n1[:], y[t][:, 0:S], ALU.add)
-                weighted_neighbours(n2, t, p2_sb, HALF, S)
-                for a in (0, HALF):
-                    nc.vector.tensor_tensor(h[t][:, a : a + HALF], part[:, a : a + HALF], n2[:, a : a + HALF], ALU.add)
-                    nc.scalar.copy(out=h_copy[t][:, a : a + HALF], in_=h[t][:, a : a + HALF])
-        for g in range(1, len(PIECES)):
-            nc.scalar.copy(out=h_last[g][:], in_=last_bank[:, PIECES[g][0] : PIECES[g][1]])
+                first_product(t, 0, S, nc.scalar.copy)
+                for a, b in HALVES:
+                    scalar_gather(first, y[t], p1_sb, a, b)
+            for a, b in HALVES:
+                nc.vector.tensor_tensor(both[:, a:b], y[t][:].indirect(entries(p2_sb, a, b)), first[:, a:b], ALU.add)
+            for a, b in HALVES:
+                nc.vector.tensor_tensor(both[:, a:b], both[:, a:b], ga_sb[:, a:b], ALU.mult)
+            for a, b in HALVES:
+                nc.vector.tensor_tensor(h[t][:, a:b], both[:, a:b], y[t][:, a:b], ALU.add)
+
+        far = [own([P, S], F32, "far%d" % t) for t in range(PACK)]
+        for t in range(PACK):
+            for a, b in HALVES:
+                scalar_gather(far[t], h[t], q1_sb, a, b)
+        z = []
+        for a, b in HALVES:
+            diff = own([P, PACK, HALF], F32, "diff%d" % a)
+            for t in range(PACK):
+                nc.vector.tensor_tensor(diff[:, t, :], h[t][:, a:b], far[t][:, a:b], ALU.subtract)
+            for c in range(a // CHUNK, b // CHUNK):
+                z.append((own([P, PACK * CHUNK], BF16, "z%d" % c), diff[:, :, c * CHUNK - a : (c + 1) * CHUNK - a]))
 
         out_word = own([P, S], U32, "out_word")
         out_scale = own([P, S], U8, "out_scale")
         out_rows = out_0.rearrange("(p t) j -> p t j", t=PACK)
         out_word_hbm = out_1[0].rearrange("p c r -> p (c r)").bitcast(I32)
-        z = [None] * CHUNKS
         result = [None] * CHUNKS
 
         def side_by_side(pairs):
@@ -218,26 +179,18 @@ def tile_picked_twohop8_gelu_po_kernel(
         def by_planes(planes):
             return planes.rearrange("p t (c i) -> p c t i", i=PACK)
 
-        def second_hop(g):
-            a, b = PIECES[g]
-            minus_d = placed([P, PACK, b - a], F32, "minus_d%d" % g, g * REGION)
-            for t in [t for t in range(PACK) if t != last_turned] + [last_turned]:
-                own_values = h_last[g][:] if t == last_turned else h_copy[t][:, a:b]
-                nc.vector.tensor_tensor(minus_d[:, t, :], h[t][:].indirect(entries(q1_sb, a, b)), own_values, ALU.subtract)
-            for c in range(a // CHUNK, b // CHUNK):
-                z[c] = own([P, PACK * CHUNK], BF16, "z%d" % c)
-                cols = slice(c * CHUNK - a, (c + 1) * CHUNK - a)
-                nc.scalar.activation(out=side_by_side(z[c][:]), in_=by_planes(minus_d[:, :, cols]), func=GELU, scale=-1.0, bias=first_bias[:] if c == 0 else zero[:, 1:2])
+        def gelu(c):
+            nc.scalar.activation(out=side_by_side(z[c][0][:]), in_=by_planes(z[c][1]), func=GELU, bias=zero[:, 1:2])
 
         def second_product(c):
             z_word = own([P, CHUNK], U32, "z_word%d" % c)
             z_scale = own([P, CHUNK], U8, "z_scale%d" % c)
-            nc.vector.quantize_mx(out=z_word[:].bitcast(FP8X4), scales=z_scale[:], in_=z[c][:])
+            nc.vector.quantize_mx(out=z_word[:].bitcast(FP8X4), scales=z_scale[:], in_=z[c][0][:])
             result[c] = own([P, PACK, CHUNK], F32, "result%d" % c)
             banks = 2 if c == CHUNKS - 1 else 1
             per_bank = PACK // banks
             for k in range(banks):
-                out_bank = product_bank([P, per_bank, CHUNK], "out_bank")
+                out_bank = bank([P, per_bank, CHUNK], "out_bank")
                 for t in range(per_bank * k, per_bank * (k + 1)):
                     nc.tensor.matmul_mx(
                         out=out_bank[:, t - per_bank * k, :],
@@ -252,25 +205,23 @@ def tile_picked_twohop8_gelu_po_kernel(
             queue = nc.scalar if c == CHUNKS - 1 else nc.sync
             queue.dma_start(out=out_rows[:, :, c * CHUNK : (c + 1) * CHUNK], in_=result[c][:])
 
-        def quantise_result(g):
-            a, b = PIECES[g]
-            rounded = own([P, PACK * (b - a)], BF16, "rounded%d" % g)
-            for c in range(a // CHUNK, b // CHUNK):
-                first = PACK * (c * CHUNK - a)
-                nc.vector.tensor_copy(out=side_by_side(rounded[:, first : first + PACK * CHUNK]), in_=by_planes(result[c][:]))
+        def quantise_result(first, end):
+            a, b = first * CHUNK, end * CHUNK
+            rounded = own([P, PACK * (b - a)], BF16, "rounded%d" % first)
+            for c in range(first, end):
+                at = PACK * (c * CHUNK - a)
+                nc.vector.tensor_copy(out=side_by_side(rounded[:, at : at + PACK * CHUNK]), in_=by_planes(result[c][:]))
             nc.vector.quantize_mx(out=out_word[:, a:b].bitcast(FP8X4), scales=out_scale[:, a:b], in_=rounded[:])
 
-        for g in range(len(PIECES) + 1):
-            if g < len(PIECES):
-                second_hop(g)
-            if g > 0:
-                for c in range(PIECES[g - 1][0] // CHUNK, PIECES[g - 1][1] // CHUNK):
-                    second_product(c)
-        for first, end in ((0, len(PIECES) - 1), (len(PIECES) - 1, len(PIECES))):
-            for g in range(first, end):
-                quantise_result(g)
-            cols = slice(PIECES[first][0], PIECES[end - 1][1])
-            nc.sync.dma_start(out=out_word_hbm[:, cols], in_=out_word[:, cols].bitcast(I32))
+        for c in range(CHUNKS):
+            gelu(c)
+        for c in range(CHUNKS):
+            second_product(c)
+        quantise_result(0, 2)
+        quantise_result(2, 3)
+        nc.sync.dma_start(out=out_word_hbm[:, 0 : 3 * CHUNK], in_=out_word[:, 0 : 3 * CHUNK].bitcast(I32))
+        quantise_result(3, 4)
+        nc.sync.dma_start(out=out_word_hbm[:, 3 * CHUNK : S], in_=out_word[:, 3 * CHUNK : S].bitcast(I32))
         for q in range(PACK):
             queue = nc.sync if q % 2 == 0 else nc.scalar
             queue.dma_start(out=out_2[0][PACK * q : PACK * (q + 1), :].bitcast(I32), in_=scale_rows(out_scale, q))

@@ -1,6 +1,7 @@
 from contextlib import ExitStack
 
 import concourse.mybir as mybir
+from concourse.masks import make_identity
 
 F32 = mybir.dt.float32
 BF16 = mybir.dt.bfloat16
@@ -25,6 +26,7 @@ LANES = 16
 QUADRANT = 32
 CHUNK = 128
 CHUNKS = S // CHUNK
+SHARE = 256
 FLOPS = 2 * H * H * S * 2
 
 
@@ -39,8 +41,8 @@ def tile_picked_twohop8_gelu_po_kernel(
         def own(shape, dtype, name):
             return keep.tile(shape, dtype, name=name, align_bytes=64)
 
-        def bank(shape, name):
-            return psum.tile(shape, F32, name=name, tag="product")
+        def bank(shape, name, tag="product"):
+            return psum.tile(shape, F32, name=name, tag=tag, bufs=7 if tag == "product" else 1)
 
         def scale_rows(tile, q):
             return tile[QUADRANT * q : QUADRANT * q + PACK, :].bitcast(I32)
@@ -57,7 +59,7 @@ def tile_picked_twohop8_gelu_po_kernel(
         w2_scale_raw = own([P, H], U8, "w2_scale_raw")
         w2_word_raw = own([P, 2 * H], U8, "w2_word_raw")
         w1_raw = [own([P, 2, H], F32, "w1_raw%d" % u) for u in range(2)]
-        ga_sb = own([P, S], F32, "ga_sb")
+        ga_sb = own([P, PACK], F32, "ga_sb")
 
         def scale_rows_apart(tile, r):
             return tile[r:P:QUADRANT, :].bitcast(I32)
@@ -73,16 +75,19 @@ def tile_picked_twohop8_gelu_po_kernel(
         nc.sync.dma_start(out=w1_raw[1][:], in_=w1_rows[:, 2:PACK, :])
         nc.sync.dma_start(p1_sb[:], p1)
         nc.sync.dma_start(p2_sb[:], p2)
-        nc.sync.dma_start(out=w2_word_raw[:].bitcast(I32), in_=w2_words[0].bitcast(I32))
+        nc.sync.dma_start(out=ga_sb[:], in_=ga[0].rearrange("(n t) -> n t", t=PACK))
         for r in range(PACK):
             queue = nc.gpsimd if r == PACK - 1 else nc.sync
             queue.dma_start(out=scale_rows_apart(w2_scale_raw, r), in_=w2_scales[0][r : PACK * PACK : PACK, :].bitcast(I32))
-        nc.sync.dma_start(out=ga_sb[:], in_=ga)
+        nc.sync.dma_start(out=w2_word_raw[:].bitcast(I32), in_=w2_words[0].bitcast(I32))
         nc.sync.dma_start(q1_sb[:], q1)
 
         zero = own([P, 2], F32, "zero")
         nc.vector.memset(zero[:, 0:1], 0.0)
         nc.scalar.activation(out=zero[:, 1:2], in_=zero[:, 0:1], func=GELU)
+
+        identity = own([P, P], F32, "identity")
+        make_identity(nc, identity[:])
 
         w1_bf = own([P, PACK * H], BF16, "w1_bf")
         w1_bf_dealt = w1_bf[:].rearrange("p (t m j) -> p m j t", t=PACK, j=PACK)
@@ -106,22 +111,17 @@ def tile_picked_twohop8_gelu_po_kernel(
         quantise_w1(1, 2)
         quantise_w1(2, PACK)
 
-        w2_word = own([P, 2 * H], U8, "w2_word")
-        nc.vector.tensor_copy(
-            out=w2_word[:].bitcast(U16).rearrange("p (t m) -> p m t", t=PACK),
-            in_=w2_word_raw[:].bitcast(U16).rearrange("p (m t) -> p m t", t=PACK),
-        )
-        w2_scale = own([P, H], U8, "w2_scale")
-        nc.vector.tensor_copy(
-            out=w2_scale[:].rearrange("p (t m) -> p m t", t=PACK),
-            in_=w2_scale_raw[:].rearrange("p (m t) -> p m t", t=PACK),
-        )
+        y = [own([P, 2 * S], F32, "y%d" % t) for t in range(PACK)]
+        h = [own([P, 2 * S], F32, "h%d" % t) for t in range(PACK)]
+        first = [own([P, S], F32, "first%d" % t) for t in range(PACK)]
+        both = [own([P, S], F32, "both%d" % t) for t in range(PACK)]
+        for t in range(PACK):
+            nc.vector.memset(y[t][:, S : 2 * S], 0.0)
 
-        y = [own([P, S], F32, "y%d" % t) for t in range(PACK)]
-        h = [own([P, S], F32, "h%d" % t) for t in range(PACK)]
+        y_banks = [None] * PACK
 
-        def first_product(t, a, b, copy):
-            y_bank = bank([P, b - a], "y_bank")
+        def first_product(t, a, b, copy, tag="product"):
+            y_bank = bank([P, b - a], "y_bank", tag)
             nc.tensor.matmul_mx(
                 out=y_bank[:],
                 lhsT=w1_word[:, P * t : P * (t + 1)].bitcast(FP8X4),
@@ -132,40 +132,75 @@ def tile_picked_twohop8_gelu_po_kernel(
                 stop=True,
             )
             copy(out=y[t][:, a:b], in_=y_bank[:])
+            y_banks[t] = (y_bank, a)
 
         def scalar_gather(dst, window, list_tile, a, b):
             nc.scalar.activation(out=dst[:, a:b], in_=window[:].indirect(entries(list_tile, a, b)), func=COPY)
 
+        def add_second(t, a, b):
+            nc.vector.tensor_tensor(both[t][:, a:b], y[t][:].indirect(entries(p2_sb, a, b)), first[t][:, a:b], ALU.add)
+
+        def weigh(t, a, b):
+            nc.vector.tensor_tensor(
+                h[t][:, S + a : S + b].rearrange("p (n t) -> p n t", t=PACK),
+                both[t][:, a:b].rearrange("p (n t) -> p n t", t=PACK),
+                ga_by_node[:, a // PACK : b // PACK, :],
+                ALU.mult,
+            )
+
+        def add_own(t, a, b):
+            y_bank, at = y_banks[t]
+            nc.vector.tensor_tensor(h[t][:, a:b], h[t][:, S + a : S + b], y_bank[:, a - at : b - at], ALU.add)
+
+        def add_own_shared(t):
+            nc.gpsimd.tensor_tensor(h[t][:, 0:SHARE], h[t][:, S : S + SHARE], y[t][:, 0:SHARE], ALU.add)
+            add_own(t, SHARE, S)
+
+        first_product(0, 0, HALF, nc.vector.tensor_copy, "early")
+        first_product(0, HALF, S, nc.scalar.copy)
+        first_product(1, 0, S, nc.scalar.copy)
+        ga_bank = bank([P, PACK, P], "ga_bank", "early")
         for t in range(PACK):
-            first = own([P, S], F32, "first%d" % t)
-            both = own([P, S], F32, "both%d" % t)
-            if t == 0:
-                first_product(t, 0, HALF, nc.scalar.copy)
-                first_product(t, HALF, S, nc.vector.tensor_copy)
-                scalar_gather(first, y[t], p1_sb, 0, HALF)
-                nc.vector.tensor_copy(out=first[:, HALF:S], in_=y[t][:].indirect(entries(p1_sb, HALF, S)))
-            else:
-                first_product(t, 0, S, nc.scalar.copy)
-                for a, b in HALVES:
-                    scalar_gather(first, y[t], p1_sb, a, b)
+            nc.tensor.transpose(ga_bank[:, t, :], ga_sb[:, t : t + 1].to_broadcast([P, P]), identity[:])
+        ga_by_node = ga_bank[:].rearrange("p t n -> p n t")
+        scalar_gather(first[0], y[0], p1_sb, 0, HALF)
+        nc.vector.tensor_copy(out=first[0][:, HALF:S], in_=y[0][:].indirect(entries(p1_sb, HALF, S)))
+        scalar_gather(first[1], y[1], p1_sb, 0, S)
+        for t in range(2, PACK):
+            first_product(t, 0, S, nc.scalar.copy)
+        for t in range(2, PACK):
+            scalar_gather(first[t], y[t], p1_sb, 0, S)
+        w2_scale = own([P, H], U8, "w2_scale")
+        nc.vector.tensor_copy(
+            out=w2_scale[:].rearrange("p (t c i) -> p c t i", t=PACK, i=16),
+            in_=w2_scale_raw[:].rearrange("p (c i t) -> p c t i", t=PACK, i=16),
+        )
+        for step in (add_second, weigh):
+            for a, b in HALVES[::-1]:
+                step(0, a, b)
+        last = PACK - 1
+        for t in range(1, PACK):
+            add_second(t, 0, S)
+            add_own_shared(t - 1)
+            if t < last:
+                weigh(t, 0, S)
+        for step in (weigh, add_own):
             for a, b in HALVES:
-                nc.vector.tensor_tensor(both[:, a:b], y[t][:].indirect(entries(p2_sb, a, b)), first[:, a:b], ALU.add)
-            for a, b in HALVES:
-                nc.vector.tensor_tensor(both[:, a:b], both[:, a:b], ga_sb[:, a:b], ALU.mult)
-            for a, b in HALVES:
-                nc.vector.tensor_tensor(h[t][:, a:b], both[:, a:b], y[t][:, a:b], ALU.add)
+                step(last, a, b)
+
+        w2_word = own([P, 2 * H], U8, "w2_word")
+        nc.scalar.copy(
+            out=w2_word[:].bitcast(U16).rearrange("p (t c i) -> p c t i", t=PACK, i=8),
+            in_=w2_word_raw[:].bitcast(U16).rearrange("p (c i t) -> p c t i", t=PACK, i=8),
+        )
 
         far = [own([P, S], F32, "far%d" % t) for t in range(PACK)]
-        for t in range(PACK):
-            for a, b in HALVES:
-                scalar_gather(far[t], h[t], q1_sb, a, b)
-        z = []
-        for a, b in HALVES:
-            diff = own([P, PACK, HALF], F32, "diff%d" % a)
-            for t in range(PACK):
-                nc.vector.tensor_tensor(diff[:, t, :], h[t][:, a:b], far[t][:, a:b], ALU.subtract)
-            for c in range(a // CHUNK, b // CHUNK):
-                z.append((own([P, PACK * CHUNK], BF16, "z%d" % c), diff[:, :, c * CHUNK - a : (c + 1) * CHUNK - a]))
+        diff = [own([P, PACK, HALF], F32, "diff%d" % u) for u in range(2)]
+        z = [own([P, PACK * CHUNK], BF16, "z%d" % c) for c in range(CHUNKS)]
+
+        def difference(u, t):
+            a, b = HALVES[u]
+            nc.vector.tensor_tensor(diff[u][:, t, :], h[t][:, a:b], far[t][:, a:b], ALU.subtract)
 
         out_word = own([P, S], U32, "out_word")
         out_scale = own([P, S], U8, "out_scale")
@@ -180,28 +215,31 @@ def tile_picked_twohop8_gelu_po_kernel(
             return planes.rearrange("p t (c i) -> p c t i", i=PACK)
 
         def gelu(c):
-            nc.scalar.activation(out=side_by_side(z[c][0][:]), in_=by_planes(z[c][1]), func=GELU, bias=zero[:, 1:2])
+            cols = slice(c % 2 * CHUNK, (c % 2 + 1) * CHUNK)
+            nc.scalar.activation(out=side_by_side(z[c][:]), in_=by_planes(diff[c // 2][:, :, cols]), func=GELU, bias=zero[:, 1:2])
 
-        def second_product(c):
-            z_word = own([P, CHUNK], U32, "z_word%d" % c)
-            z_scale = own([P, CHUNK], U8, "z_scale%d" % c)
-            nc.vector.quantize_mx(out=z_word[:].bitcast(FP8X4), scales=z_scale[:], in_=z[c][0][:])
+        z_word = [own([P, CHUNK], U32, "z_word%d" % c) for c in range(CHUNKS)]
+        z_scale = [own([P, CHUNK], U8, "z_scale%d" % c) for c in range(CHUNKS)]
+
+        def quantise_z(c):
+            nc.vector.quantize_mx(out=z_word[c][:].bitcast(FP8X4), scales=z_scale[c][:], in_=z[c][:])
+
+        def second_product(c, copies):
             result[c] = own([P, PACK, CHUNK], F32, "result%d" % c)
-            banks = 2 if c == CHUNKS - 1 else 1
-            per_bank = PACK // banks
-            for k in range(banks):
+            per_bank = PACK // len(copies)
+            for k, copy in enumerate(copies):
                 out_bank = bank([P, per_bank, CHUNK], "out_bank")
                 for t in range(per_bank * k, per_bank * (k + 1)):
                     nc.tensor.matmul_mx(
                         out=out_bank[:, t - per_bank * k, :],
                         lhsT=w2_word[:, 2 * P * t : 2 * P * (t + 1)].bitcast(FP4X4),
                         lhsT_scale=w2_scale[:, P * t : P * (t + 1)],
-                        rhs=z_word[:].bitcast(FP8X4),
-                        rhs_scale=z_scale[:],
+                        rhs=z_word[c][:].bitcast(FP8X4),
+                        rhs_scale=z_scale[c][:],
                         start=True,
                         stop=True,
                     )
-                nc.scalar.copy(out=result[c][:, per_bank * k : per_bank * (k + 1), :], in_=out_bank[:])
+                copy(out=result[c][:, per_bank * k : per_bank * (k + 1), :], in_=out_bank[:])
             queue = nc.scalar if c == CHUNKS - 1 else nc.sync
             queue.dma_start(out=out_rows[:, :, c * CHUNK : (c + 1) * CHUNK], in_=result[c][:])
 
@@ -213,10 +251,27 @@ def tile_picked_twohop8_gelu_po_kernel(
                 nc.vector.tensor_copy(out=side_by_side(rounded[:, at : at + PACK * CHUNK]), in_=by_planes(result[c][:]))
             nc.vector.quantize_mx(out=out_word[:, a:b].bitcast(FP8X4), scales=out_scale[:, a:b], in_=rounded[:])
 
-        for c in range(CHUNKS):
-            gelu(c)
-        for c in range(CHUNKS):
-            second_product(c)
+        for t in range(PACK - 1):
+            scalar_gather(far[t], h[t], q1_sb, 0, S)
+        for a, b in HALVES:
+            scalar_gather(far[PACK - 1], h[PACK - 1], q1_sb, a, b)
+        for t in range(PACK):
+            difference(0, t)
+        gelu(0)
+        gelu(1)
+        for t in range(PACK - 1):
+            difference(1, t)
+        quantise_z(0)
+        difference(1, PACK - 1)
+        quantise_z(1)
+        gelu(2)
+        gelu(3)
+        quantise_z(2)
+        second_product(0, [nc.vector.tensor_copy])
+        quantise_z(3)
+        second_product(1, [nc.scalar.copy])
+        second_product(2, [nc.scalar.copy])
+        second_product(3, [nc.scalar.copy, nc.scalar.copy])
         quantise_result(0, 2)
         quantise_result(2, 3)
         nc.sync.dma_start(out=out_word_hbm[:, 0 : 3 * CHUNK], in_=out_word[:, 0 : 3 * CHUNK].bitcast(I32))

@@ -36,10 +36,14 @@ def tile_picked_twohop8_gelu_po_kernel(
     nc = tc.nc
     with ExitStack() as ctx:
         keep = ctx.enter_context(tc.tile_pool(name="keep", bufs=1))
+        shared = ctx.enter_context(tc.tile_pool(name="shared", bufs=1))
         psum = ctx.enter_context(tc.psum_pool(name="psum", bufs=8))
 
         def own(shape, dtype, name):
             return keep.tile(shape, dtype, name=name, align_bytes=64)
+
+        def placed(shape, dtype, name, offset):
+            return shared.tile(shape, dtype, name=name, offset=offset, align_bytes=64)
 
         def bank(shape, name, tag="product"):
             return psum.tile(shape, F32, name=name, tag=tag, bufs=7 if tag == "product" else 1)
@@ -112,13 +116,15 @@ def tile_picked_twohop8_gelu_po_kernel(
         quantise_w1(2, PACK)
 
         y = [own([P, 2 * S], F32, "y%d" % t) for t in range(PACK)]
-        h = [own([P, 2 * S], F32, "h%d" % t) for t in range(PACK)]
-        first = [own([P, S], F32, "first%d" % t) for t in range(PACK)]
-        both = [own([P, S], F32, "both%d" % t) for t in range(PACK)]
+        last = PACK - 1
+        h = [own([P, S if t == last else 2 * S], F32, "h%d" % t) for t in range(PACK)]
+        weighted = [own([P, S], F32, "weighted3")[:] if t == last else h[t][:, S : 2 * S] for t in range(PACK)]
+        first = [placed([P, S], F32, "first3", 0) if t == PACK - 1 else own([P, S], F32, "first%d" % t) for t in range(PACK)]
+        both = [placed([P, S], F32, "both3", 8 * S) if t == PACK - 1 else own([P, S], F32, "both%d" % t) for t in range(PACK)]
         for t in range(PACK):
             nc.vector.memset(y[t][:, S : 2 * S], 0.0)
 
-        y_banks = [None] * PACK
+        y_banks = [[] for t in range(PACK)]
 
         def first_product(t, a, b, copy, tag="product"):
             y_bank = bank([P, b - a], "y_bank", tag)
@@ -132,7 +138,7 @@ def tile_picked_twohop8_gelu_po_kernel(
                 stop=True,
             )
             copy(out=y[t][:, a:b], in_=y_bank[:])
-            y_banks[t] = (y_bank, a)
+            y_banks[t].append((y_bank, a, b))
 
         def scalar_gather(dst, window, list_tile, a, b):
             nc.scalar.activation(out=dst[:, a:b], in_=window[:].indirect(entries(list_tile, a, b)), func=COPY)
@@ -142,22 +148,26 @@ def tile_picked_twohop8_gelu_po_kernel(
 
         def weigh(t, a, b):
             nc.vector.tensor_tensor(
-                h[t][:, S + a : S + b].rearrange("p (n t) -> p n t", t=PACK),
+                weighted[t][:, a:b].rearrange("p (n t) -> p n t", t=PACK),
                 both[t][:, a:b].rearrange("p (n t) -> p n t", t=PACK),
                 ga_by_node[:, a // PACK : b // PACK, :],
                 ALU.mult,
             )
 
         def add_own(t, a, b):
-            y_bank, at = y_banks[t]
-            nc.vector.tensor_tensor(h[t][:, a:b], h[t][:, S + a : S + b], y_bank[:, a - at : b - at], ALU.add)
+            for y_bank, start, end in y_banks[t]:
+                lo, hi = max(a, start), min(b, end)
+                if lo < hi:
+                    nc.vector.tensor_tensor(h[t][:, lo:hi], weighted[t][:, lo:hi], y_bank[:, lo - start : hi - start], ALU.add)
 
         def add_own_shared(t):
             nc.gpsimd.tensor_tensor(h[t][:, 0:SHARE], h[t][:, S : S + SHARE], y[t][:, 0:SHARE], ALU.add)
             add_own(t, SHARE, S)
 
-        first_product(0, 0, HALF, nc.vector.tensor_copy, "early")
-        first_product(0, HALF, S, nc.scalar.copy)
+        first_product(0, 0, CHUNK, nc.scalar.copy, "early")
+        first_product(0, CHUNK, HALF, nc.scalar.copy)
+        first_product(0, HALF, HALF + CHUNK, nc.vector.tensor_copy)
+        first_product(0, HALF + CHUNK, S, nc.scalar.copy)
         first_product(1, 0, S, nc.scalar.copy)
         ga_bank = bank([P, PACK, P], "ga_bank", "early")
         for t in range(PACK):
@@ -178,7 +188,6 @@ def tile_picked_twohop8_gelu_po_kernel(
         for step in (add_second, weigh):
             for a, b in HALVES[::-1]:
                 step(0, a, b)
-        last = PACK - 1
         for t in range(1, PACK):
             add_second(t, 0, S)
             add_own_shared(t - 1)
@@ -188,19 +197,19 @@ def tile_picked_twohop8_gelu_po_kernel(
             for a, b in HALVES:
                 step(last, a, b)
 
-        w2_word = own([P, 2 * H], U8, "w2_word")
-        nc.scalar.copy(
+        w2_word = placed([P, 2 * H], U8, "w2_word", 8 * S)
+        nc.vector.tensor_copy(
             out=w2_word[:].bitcast(U16).rearrange("p (t c i) -> p c t i", t=PACK, i=8),
             in_=w2_word_raw[:].bitcast(U16).rearrange("p (c i t) -> p c t i", t=PACK, i=8),
         )
 
-        far = [own([P, S], F32, "far%d" % t) for t in range(PACK)]
-        diff = [own([P, PACK, HALF], F32, "diff%d" % u) for u in range(2)]
+        far = [own([P, S], F32, "far%d" % t) for t in range(last)]
+        diff = [placed([P, PACK, HALF], F32, "diff0", 0), own([P, PACK, HALF], F32, "diff1")]
         z = [own([P, PACK * CHUNK], BF16, "z%d" % c) for c in range(CHUNKS)]
 
-        def difference(u, t):
+        def difference(u, t, engine=nc.vector):
             a, b = HALVES[u]
-            nc.vector.tensor_tensor(diff[u][:, t, :], h[t][:, a:b], far[t][:, a:b], ALU.subtract)
+            engine.tensor_tensor(diff[u][:, t, :], h[t][:, a:b], far[t][:, a:b], ALU.subtract)
 
         out_word = own([P, S], U32, "out_word")
         out_scale = own([P, S], U8, "out_scale")
@@ -253,17 +262,35 @@ def tile_picked_twohop8_gelu_po_kernel(
 
         for t in range(PACK - 1):
             scalar_gather(far[t], h[t], q1_sb, 0, S)
-        for a, b in HALVES:
-            scalar_gather(far[PACK - 1], h[PACK - 1], q1_sb, a, b)
-        for t in range(PACK):
+        far_last = [None] * CHUNKS
+
+        def last_gather(c):
+            far_last[c] = keep.tile([P, CHUNK], F32, name="far_last", bufs=2)
+            a = c * CHUNK
+            nc.scalar.activation(out=far_last[c][:], in_=h[last][:].indirect(entries(q1_sb, a, a + CHUNK)), func=COPY)
+
+        def last_difference(c):
+            a = c * CHUNK
+            nc.vector.tensor_tensor(diff[c // 2][:, last, a % HALF : a % HALF + CHUNK], h[last][:, a : a + CHUNK], far_last[c][:], ALU.subtract)
+
+        last_gather(0)
+        last_gather(1)
+        difference(0, 0, nc.gpsimd)
+        for t in range(1, last):
             difference(0, t)
+        last_difference(0)
+        last_difference(1)
         gelu(0)
+        last_gather(2)
         gelu(1)
-        for t in range(PACK - 1):
-            difference(1, t)
+        last_gather(3)
+        difference(1, 0)
+        difference(1, 1)
         quantise_z(0)
-        difference(1, PACK - 1)
+        difference(1, 2)
+        last_difference(2)
         quantise_z(1)
+        last_difference(3)
         gelu(2)
         gelu(3)
         quantise_z(2)
@@ -271,11 +298,17 @@ def tile_picked_twohop8_gelu_po_kernel(
         quantise_z(3)
         second_product(1, [nc.scalar.copy])
         second_product(2, [nc.scalar.copy])
-        second_product(3, [nc.scalar.copy, nc.scalar.copy])
+        second_product(3, [nc.scalar.copy] * PACK)
         quantise_result(0, 2)
         quantise_result(2, 3)
         nc.sync.dma_start(out=out_word_hbm[:, 0 : 3 * CHUNK], in_=out_word[:, 0 : 3 * CHUNK].bitcast(I32))
-        quantise_result(3, 4)
+        rounded = own([P, PACK * CHUNK], BF16, "rounded_last")
+        piece = CHUNK // 2
+        for a in (0, piece):
+            nc.vector.tensor_copy(out=side_by_side(rounded[:, PACK * a : PACK * (a + piece)]), in_=by_planes(result[3][:, :, a : a + piece]))
+        for a in (0, piece):
+            cols = slice(3 * CHUNK + a, 3 * CHUNK + a + piece)
+            nc.vector.quantize_mx(out=out_word[:, cols].bitcast(FP8X4), scales=out_scale[:, cols], in_=rounded[:, PACK * a : PACK * (a + piece)])
         nc.sync.dma_start(out=out_word_hbm[:, 3 * CHUNK : S], in_=out_word[:, 3 * CHUNK : S].bitcast(I32))
         for q in range(PACK):
             queue = nc.sync if q % 2 == 0 else nc.scalar

@@ -27,6 +27,7 @@ QUADRANT = 32
 CHUNK = 128
 CHUNKS = S // CHUNK
 SHARE = 256
+SHORT_SHARE = 160
 FLOPS = 2 * H * H * S * 2
 
 
@@ -161,8 +162,9 @@ def tile_picked_twohop8_gelu_po_kernel(
                     nc.vector.tensor_tensor(h[t][:, lo:hi], weighted[t][:, lo:hi], y_bank[:, lo - start : hi - start], ALU.add)
 
         def add_own_shared(t):
-            nc.gpsimd.tensor_tensor(h[t][:, 0:SHARE], h[t][:, S : S + SHARE], y[t][:, 0:SHARE], ALU.add)
-            add_own(t, SHARE, S)
+            share = SHORT_SHARE if t == last - 1 else SHARE
+            nc.gpsimd.tensor_tensor(h[t][:, 0:share], h[t][:, S : S + share], y[t][:, 0:share], ALU.add)
+            add_own(t, share, S)
 
         first_product(0, 0, CHUNK, nc.scalar.copy, "early")
         first_product(0, CHUNK, HALF, nc.scalar.copy)

@@ -267,32 +267,33 @@ def tile_picked_twohop8_gelu_po_kernel(
         far_last = [None] * CHUNKS
 
         def last_gather(c):
-            far_last[c] = keep.tile([P, CHUNK], F32, name="far_last", bufs=2)
-            a = c * CHUNK
-            nc.scalar.activation(out=far_last[c][:], in_=h[last][:].indirect(entries(q1_sb, a, a + CHUNK)), func=COPY)
+            far_last[c] = own([P, CHUNK], F32, "far_last%d" % c)
+            window = h[last][:].indirect(entries(q1_sb, c * CHUNK, (c + 1) * CHUNK))
+            if c == 0:
+                nc.vector.tensor_copy(out=far_last[c][:], in_=window)
+            else:
+                nc.scalar.activation(out=far_last[c][:], in_=window, func=COPY)
 
         def last_difference(c):
             a = c * CHUNK
             nc.vector.tensor_tensor(diff[c // 2][:, last, a % HALF : a % HALF + CHUNK], h[last][:, a : a + CHUNK], far_last[c][:], ALU.subtract)
 
-        last_gather(0)
-        last_gather(1)
+        for c in range(CHUNKS):
+            last_gather(c)
         difference(0, 0, nc.gpsimd)
         for t in range(1, last):
             difference(0, t)
         last_difference(0)
         last_difference(1)
         gelu(0)
-        last_gather(2)
         gelu(1)
-        last_gather(3)
         difference(1, 0)
-        difference(1, 1)
         quantise_z(0)
+        difference(1, 1)
         difference(1, 2)
         last_difference(2)
-        quantise_z(1)
         last_difference(3)
+        quantise_z(1)
         gelu(2)
         gelu(3)
         quantise_z(2)

@@ -297,7 +297,7 @@ def tile_picked_twohop8_gelu_po_kernel(
         gelu(2)
         gelu(3)
         quantise_z(2)
-        second_product(0, [nc.vector.tensor_copy])
+        second_product(0, [nc.scalar.copy])
         quantise_z(3)
         second_product(1, [nc.scalar.copy])
         second_product(2, [nc.scalar.copy])

@@ -200,10 +200,12 @@ def tile_picked_twohop8_gelu_po_kernel(
                 step(last, a, b)
 
         w2_word = placed([P, 2 * H], U8, "w2_word", 8 * S)
-        nc.vector.tensor_copy(
-            out=w2_word[:].bitcast(U16).rearrange("p (t c i) -> p c t i", t=PACK, i=8),
-            in_=w2_word_raw[:].bitcast(U16).rearrange("p (c i t) -> p c t i", t=PACK, i=8),
-        )
+
+        def deal_w2_words():
+            nc.vector.tensor_copy(
+                out=w2_word[:].bitcast(U16).rearrange("p (t c i) -> p c t i", t=PACK, i=8),
+                in_=w2_word_raw[:].bitcast(U16).rearrange("p (c i t) -> p c t i", t=PACK, i=8),
+            )
 
         far = [own([P, S], F32, "far%d" % t) for t in range(last)]
         diff = [placed([P, PACK, HALF], F32, "diff0", 0), own([P, PACK, HALF], F32, "diff1")]
@@ -278,18 +280,19 @@ def tile_picked_twohop8_gelu_po_kernel(
             a = c * CHUNK
             nc.vector.tensor_tensor(diff[c // 2][:, last, a % HALF : a % HALF + CHUNK], h[last][:, a : a + CHUNK], far_last[c][:], ALU.subtract)
 
+        difference(0, 0, nc.gpsimd)
+        difference(0, 1)
         for c in range(CHUNKS):
             last_gather(c)
-        difference(0, 0, nc.gpsimd)
-        for t in range(1, last):
-            difference(0, t)
+        difference(1, 0)
+        difference(0, 2)
         last_difference(0)
         last_difference(1)
+        deal_w2_words()
         gelu(0)
         gelu(1)
-        difference(1, 0)
-        quantise_z(0)
         difference(1, 1)
+        quantise_z(0)
         difference(1, 2)
         last_difference(2)
         last_difference(3)
@@ -297,7 +300,7 @@ def tile_picked_twohop8_gelu_po_kernel(
         gelu(2)
         gelu(3)
         quantise_z(2)
-        second_product(0, [nc.scalar.copy])
+        second_product(0, [nc.vector.tensor_copy, nc.scalar.copy])
         quantise_z(3)
         second_product(1, [nc.scalar.copy])
         second_product(2, [nc.scalar.copy])

from contextlib import ExitStack

import concourse.mybir as mybir
from concourse.masks import make_identity

F32 = mybir.dt.float32
BF16 = mybir.dt.bfloat16
I32 = mybir.dt.int32
U32 = mybir.dt.uint32
U16 = mybir.dt.uint16
U8 = mybir.dt.uint8
FP8X4 = mybir.dt.float8_e4m3fn_x4
FP4X4 = mybir.dt.float4_e2m1fn_x4
ALU = mybir.AluOpType
GELU = mybir.ActivationFunctionType.Gelu_apprx_tanh
COPY = mybir.ActivationFunctionType.Copy

P = 128
PACK = 4
T = 2048
S = 512
H = 512
HALF = S // 2
HALVES = ((0, HALF), (HALF, S))
LANES = 16
QUADRANT = 32
CHUNK = 128
CHUNKS = S // CHUNK
SHARE = 256
SHORT_SHARE = 160
FLOPS = 2 * H * H * S * 2


def tile_picked_twohop8_gelu_po_kernel(
    tc, x_words, x_scales, w1, ga, w2_words, w2_scales, offs, p1, p2, q1, out_0, out_1, out_2
):
    nc = tc.nc
    with ExitStack() as ctx:
        keep = ctx.enter_context(tc.tile_pool(name="keep", bufs=1))
        shared = ctx.enter_context(tc.tile_pool(name="shared", bufs=1))
        psum = ctx.enter_context(tc.psum_pool(name="psum", bufs=8))

        def own(shape, dtype, name):
            return keep.tile(shape, dtype, name=name, align_bytes=64)

        def placed(shape, dtype, name, offset):
            return shared.tile(shape, dtype, name=name, offset=offset, align_bytes=64)

        def bank(shape, name, tag="product"):
            return psum.tile(shape, F32, name=name, tag=tag, bufs=7 if tag == "product" else 1)

        def scale_rows(tile, q):
            return tile[QUADRANT * q : QUADRANT * q + PACK, :].bitcast(I32)

        def entries(list_tile, a, b):
            return list_tile[:, a // LANES : b // LANES]

        offs_sb = keep.tile([P, S // LANES], U16, name="offs_sb")
        p1_sb = keep.tile([P, S // LANES], U16, name="p1_sb")
        p2_sb = keep.tile([P, S // LANES], U16, name="p2_sb")
        q1_sb = keep.tile([P, S // LANES], U16, name="q1_sb")
        x_scale_table = own([P, T], U8, "x_scale_table")
        x_word_table = own([P, T], U32, "x_word_table")
        w2_scale_raw = own([P, H], U8, "w2_scale_raw")
        w2_word_raw = own([P, 2 * H], U8, "w2_word_raw")
        w1_raw = [own([P, 2, H], F32, "w1_raw%d" % u) for u in range(2)]
        ga_sb = own([P, PACK], F32, "ga_sb")

        def scale_rows_apart(tile, r):
            return tile[r:P:QUADRANT, :].bitcast(I32)

        nc.vector.memset(x_scale_table[:].bitcast(I32), 0)
        nc.vector.memset(w2_scale_raw[:].bitcast(I32), 0)
        w1_rows = w1.rearrange("(p j) c -> p j c", j=PACK)
        nc.sync.dma_start(out=w1_raw[0][:], in_=w1_rows[:, 0:2, :])
        for r in range(PACK):
            nc.sync.dma_start(out=scale_rows_apart(x_scale_table, r), in_=x_scales[0][r : PACK * PACK : PACK, :].bitcast(I32))
        nc.sync.dma_start(offs_sb[:], offs)
        nc.sync.dma_start(out=x_word_table[:].bitcast(I32), in_=x_words[0].rearrange("p c r -> p (c r)").bitcast(I32))
        nc.sync.dma_start(out=w1_raw[1][:], in_=w1_rows[:, 2:PACK, :])
        nc.sync.dma_start(p1_sb[:], p1)
        nc.sync.dma_start(p2_sb[:], p2)
        nc.sync.dma_start(out=ga_sb[:], in_=ga[0].rearrange("(n t) -> n t", t=PACK))
        for r in range(PACK):
            queue = nc.gpsimd if r == PACK - 1 else nc.sync
            queue.dma_start(out=scale_rows_apart(w2_scale_raw, r), in_=w2_scales[0][r : PACK * PACK : PACK, :].bitcast(I32))
        nc.sync.dma_start(out=w2_word_raw[:].bitcast(I32), in_=w2_words[0].bitcast(I32))
        nc.sync.dma_start(q1_sb[:], q1)

        zero = own([P, 2], F32, "zero")
        nc.vector.memset(zero[:, 0:1], 0.0)
        nc.scalar.activation(out=zero[:, 1:2], in_=zero[:, 0:1], func=GELU)

        identity = own([P, P], F32, "identity")
        make_identity(nc, identity[:])

        w1_bf = own([P, PACK * H], BF16, "w1_bf")
        w1_bf_dealt = w1_bf[:].rearrange("p (t m j) -> p m j t", t=PACK, j=PACK)
        x_scale = own([P, S], U8, "x_scale")
        nc.vector.tensor_copy(out=x_scale[:], in_=x_scale_table[:].indirect(offs_sb[:]))
        by_column = [raw[:].rearrange("p j (m t) -> p m j t", t=PACK) for raw in w1_raw]
        nc.vector.tensor_copy(out=w1_bf_dealt[:, :, 0:2], in_=by_column[0])
        x_word = own([P, S], U32, "x_word")
        nc.vector.tensor_copy(out=x_word[:], in_=x_word_table[:].indirect(offs_sb[:]))
        w1_word = own([P, H], U32, "w1_word")
        w1_scale = own([P, H], U8, "w1_scale")

        def quantise_w1(first, end):
            a, b = P * first, P * end
            nc.vector.quantize_mx(out=w1_word[:, a:b].bitcast(FP8X4), scales=w1_scale[:, a:b], in_=w1_bf[:, PACK * a : PACK * b])

        for t in (0, 1):
            nc.vector.tensor_copy(out=w1_bf_dealt[:, :, 2:PACK, t], in_=by_column[1][:, :, :, t])
        nc.scalar.copy(out=w1_bf_dealt[:, :, 2:PACK, 2:PACK], in_=by_column[1][:, :, :, 2:PACK])
        quantise_w1(0, 1)
        quantise_w1(1, 2)
        quantise_w1(2, PACK)

        y = [own([P, 2 * S], F32, "y%d" % t) for t in range(PACK)]
        last = PACK - 1
        h = [own([P, S if t == last else 2 * S], F32, "h%d" % t) for t in range(PACK)]
        weighted = [own([P, S], F32, "weighted3")[:] if t == last else h[t][:, S : 2 * S] for t in range(PACK)]
        first = [placed([P, S], F32, "first3", 0) if t == PACK - 1 else own([P, S], F32, "first%d" % t) for t in range(PACK)]
        both = [placed([P, S], F32, "both3", 8 * S) if t == PACK - 1 else own([P, S], F32, "both%d" % t) for t in range(PACK)]
        for t in range(PACK):
            nc.vector.memset(y[t][:, S : 2 * S], 0.0)

        y_banks = [[] for t in range(PACK)]

        def first_product(t, a, b, copy, tag="product"):
            y_bank = bank([P, b - a], "y_bank", tag)
            nc.tensor.matmul_mx(
                out=y_bank[:],
                lhsT=w1_word[:, P * t : P * (t + 1)].bitcast(FP8X4),
                lhsT_scale=w1_scale[:, P * t : P * (t + 1)],
                rhs=x_word[:, a:b].bitcast(FP8X4),
                rhs_scale=x_scale[:, a:b],
                start=True,
                stop=True,
            )
            copy(out=y[t][:, a:b], in_=y_bank[:])
            y_banks[t].append((y_bank, a, b))

        def scalar_gather(dst, window, list_tile, a, b):
            nc.scalar.activation(out=dst[:, a:b], in_=window[:].indirect(entries(list_tile, a, b)), func=COPY)

        def add_second(t, a, b):
            nc.vector.tensor_tensor(both[t][:, a:b], y[t][:].indirect(entries(p2_sb, a, b)), first[t][:, a:b], ALU.add)

        def weigh(t, a, b):
            nc.vector.tensor_tensor(
                weighted[t][:, a:b].rearrange("p (n t) -> p n t", t=PACK),
                both[t][:, a:b].rearrange("p (n t) -> p n t", t=PACK),
                ga_by_node[:, a // PACK : b // PACK, :],
                ALU.mult,
            )

        def add_own(t, a, b):
            for y_bank, start, end in y_banks[t]:
                lo, hi = max(a, start), min(b, end)
                if lo < hi:
                    nc.vector.tensor_tensor(h[t][:, lo:hi], weighted[t][:, lo:hi], y_bank[:, lo - start : hi - start], ALU.add)

        def add_own_shared(t):
            share = SHORT_SHARE if t == last - 1 else SHARE
            nc.gpsimd.tensor_tensor(h[t][:, 0:share], h[t][:, S : S + share], y[t][:, 0:share], ALU.add)
            add_own(t, share, S)

        first_product(0, 0, CHUNK, nc.scalar.copy, "early")
        first_product(0, CHUNK, HALF, nc.scalar.copy)
        first_product(0, HALF, HALF + CHUNK, nc.vector.tensor_copy)
        first_product(0, HALF + CHUNK, S, nc.scalar.copy)
        first_product(1, 0, S, nc.scalar.copy)
        ga_bank = bank([P, PACK, P], "ga_bank", "early")
        for t in range(PACK):
            nc.tensor.transpose(ga_bank[:, t, :], ga_sb[:, t : t + 1].to_broadcast([P, P]), identity[:])
        ga_by_node = ga_bank[:].rearrange("p t n -> p n t")
        scalar_gather(first[0], y[0], p1_sb, 0, HALF)
        nc.vector.tensor_copy(out=first[0][:, HALF:S], in_=y[0][:].indirect(entries(p1_sb, HALF, S)))
        scalar_gather(first[1], y[1], p1_sb, 0, S)
        for t in range(2, PACK):
            first_product(t, 0, S, nc.scalar.copy)
        for t in range(2, PACK):
            scalar_gather(first[t], y[t], p1_sb, 0, S)
        w2_scale = own([P, H], U8, "w2_scale")
        nc.vector.tensor_copy(
            out=w2_scale[:].rearrange("p (t c i) -> p c t i", t=PACK, i=16),
            in_=w2_scale_raw[:].rearrange("p (c i t) -> p c t i", t=PACK, i=16),
        )
        for step in (add_second, weigh):
            for a, b in HALVES[::-1]:
                step(0, a, b)
        for t in range(1, PACK):
            add_second(t, 0, S)
            add_own_shared(t - 1)
            if t < last:
                weigh(t, 0, S)
        for step in (weigh, add_own):
            for a, b in HALVES:
                step(last, a, b)

        w2_word = placed([P, 2 * H], U8, "w2_word", 8 * S)

        def deal_w2_words():
            nc.vector.tensor_copy(
                out=w2_word[:].bitcast(U16).rearrange("p (t c i) -> p c t i", t=PACK, i=8),
                in_=w2_word_raw[:].bitcast(U16).rearrange("p (c i t) -> p c t i", t=PACK, i=8),
            )

        far = [own([P, S], F32, "far%d" % t) for t in range(last)]
        diff = [placed([P, PACK, HALF], F32, "diff0", 0), own([P, PACK, HALF], F32, "diff1")]
        z = [own([P, PACK * CHUNK], BF16, "z%d" % c) for c in range(CHUNKS)]

        def difference(u, t, engine=nc.vector):
            a, b = HALVES[u]
            engine.tensor_tensor(diff[u][:, t, :], h[t][:, a:b], far[t][:, a:b], ALU.subtract)

        out_word = own([P, S], U32, "out_word")
        out_scale = own([P, S], U8, "out_scale")
        out_rows = out_0.rearrange("(p t) j -> p t j", t=PACK)
        out_word_hbm = out_1[0].rearrange("p c r -> p (c r)").bitcast(I32)
        result = [None] * CHUNKS

        def side_by_side(pairs):
            return pairs.rearrange("p (c i t) -> p c t i", i=PACK, t=PACK)

        def by_planes(planes):
            return planes.rearrange("p t (c i) -> p c t i", i=PACK)

        def gelu(c):
            cols = slice(c % 2 * CHUNK, (c % 2 + 1) * CHUNK)
            nc.scalar.activation(out=side_by_side(z[c][:]), in_=by_planes(diff[c // 2][:, :, cols]), func=GELU, bias=zero[:, 1:2])

        z_word = [own([P, CHUNK], U32, "z_word%d" % c) for c in range(CHUNKS)]
        z_scale = [own([P, CHUNK], U8, "z_scale%d" % c) for c in range(CHUNKS)]

        def quantise_z(c):
            nc.vector.quantize_mx(out=z_word[c][:].bitcast(FP8X4), scales=z_scale[c][:], in_=z[c][:])

        def second_product(c, copies):
            result[c] = own([P, PACK, CHUNK], F32, "result%d" % c)
            per_bank = PACK // len(copies)
            for k, copy in enumerate(copies):
                out_bank = bank([P, per_bank, CHUNK], "out_bank")
                for t in range(per_bank * k, per_bank * (k + 1)):
                    nc.tensor.matmul_mx(
                        out=out_bank[:, t - per_bank * k, :],
                        lhsT=w2_word[:, 2 * P * t : 2 * P * (t + 1)].bitcast(FP4X4),
                        lhsT_scale=w2_scale[:, P * t : P * (t + 1)],
                        rhs=z_word[c][:].bitcast(FP8X4),
                        rhs_scale=z_scale[c][:],
                        start=True,
                        stop=True,
                    )
                copy(out=result[c][:, per_bank * k : per_bank * (k + 1), :], in_=out_bank[:])
            queue = nc.scalar if c == CHUNKS - 1 else nc.sync
            queue.dma_start(out=out_rows[:, :, c * CHUNK : (c + 1) * CHUNK], in_=result[c][:])

        def quantise_result(first, end):
            a, b = first * CHUNK, end * CHUNK
            rounded = own([P, PACK * (b - a)], BF16, "rounded%d" % first)
            for c in range(first, end):
                at = PACK * (c * CHUNK - a)
                nc.vector.tensor_copy(out=side_by_side(rounded[:, at : at + PACK * CHUNK]), in_=by_planes(result[c][:]))
            nc.vector.quantize_mx(out=out_word[:, a:b].bitcast(FP8X4), scales=out_scale[:, a:b], in_=rounded[:])

        for t in range(PACK - 1):
            scalar_gather(far[t], h[t], q1_sb, 0, S)
        far_last = [None] * CHUNKS

        def last_gather(c):
            far_last[c] = own([P, CHUNK], F32, "far_last%d" % c)
            window = h[last][:].indirect(entries(q1_sb, c * CHUNK, (c + 1) * CHUNK))
            if c == 0:
                nc.vector.tensor_copy(out=far_last[c][:], in_=window)
            else:
                nc.scalar.activation(out=far_last[c][:], in_=window, func=COPY)

        def last_difference(c):
            a = c * CHUNK
            nc.vector.tensor_tensor(diff[c // 2][:, last, a % HALF : a % HALF + CHUNK], h[last][:, a : a + CHUNK], far_last[c][:], ALU.subtract)

        difference(0, 0, nc.gpsimd)
        difference(0, 1)
        for c in range(CHUNKS):
            last_gather(c)
        difference(1, 0)
        difference(0, 2)
        last_difference(0)
        last_difference(1)
        deal_w2_words()
        gelu(0)
        gelu(1)
        difference(1, 1)
        quantise_z(0)
        difference(1, 2)
        last_difference(2)
        last_difference(3)
        quantise_z(1)
        gelu(2)
        gelu(3)
        quantise_z(2)
        second_product(0, [nc.vector.tensor_copy, nc.scalar.copy])
        quantise_z(3)
        second_product(1, [nc.scalar.copy])
        second_product(2, [nc.scalar.copy])
        second_product(3, [nc.scalar.copy] * PACK)
        quantise_result(0, 2)
        quantise_result(2, 3)
        nc.sync.dma_start(out=out_word_hbm[:, 0 : 3 * CHUNK], in_=out_word[:, 0 : 3 * CHUNK].bitcast(I32))
        rounded = own([P, PACK * CHUNK], BF16, "rounded_last")
        piece = CHUNK // 2
        for a in (0, piece):
            nc.vector.tensor_copy(out=side_by_side(rounded[:, PACK * a : PACK * (a + piece)]), in_=by_planes(result[3][:, :, a : a + piece]))
        for a in (0, piece):
            cols = slice(3 * CHUNK + a, 3 * CHUNK + a + piece)
            nc.vector.quantize_mx(out=out_word[:, cols].bitcast(FP8X4), scales=out_scale[:, cols], in_=rounded[:, PACK * a : PACK * (a + piece)])
        nc.sync.dma_start(out=out_word_hbm[:, 3 * CHUNK : S], in_=out_word[:, 3 * CHUNK : S].bitcast(I32))
        for q in range(PACK):
            queue = nc.sync if q % 2 == 0 else nc.scalar
            queue.dma_start(out=out_2[0][PACK * q : PACK * (q + 1), :].bitcast(I32), in_=scale_rows(out_scale, q))
